import numpy as np
import ml_dtypes


def mxq(x, axis, fmt="e4m3"):
    dtype, down = {"e4m3": (ml_dtypes.float8_e4m3fn, 7), "e5m2": (ml_dtypes.float8_e5m2, 14)}[fmt]
    v = np.moveaxis(np.asarray(x, np.float32).astype(ml_dtypes.bfloat16).astype(np.float64), axis, -1)
    blocks = v.reshape(v.shape[:-1] + (-1, 32))
    amax = np.abs(blocks).max(-1, keepdims=True)
    byte = np.maximum(np.where(amax > 0, np.frexp(amax)[1] - 1 + 127, 0) - down, 1)
    scale = np.exp2(byte - 127.0)
    codes = (blocks / scale).astype(np.float32).astype(dtype).astype(np.float64)
    return np.moveaxis((codes * scale).reshape(v.shape), -1, axis)


WIDE = False


def mx_kscale(k):
    if not WIDE:
        return np.ones(k)
    levels = np.array([10, -10, 5, -5, 0])
    if k % 512:
        return np.exp2(np.random.permutation(np.resize(levels, k // 32))).repeat(32)
    a = np.empty((k // 512, 16))
    for p in range(k // 512):
        a[p, :8] = np.random.permutation(np.resize(levels, 8))
        for g in range(8):
            far = levels[np.abs(levels - a[p, g]) >= 10]
            a[p, g + 8] = far[np.random.randint(len(far))]
    return np.exp2(a.ravel()).repeat(32)


def f64(x):
    return np.asarray(x).astype(np.float64)


def striped(idx):
    return np.tile(idx.reshape(-1, 16).T, (8, 1)).astype(np.uint16)


def unstriped(offs):
    return offs[:16].T.reshape(-1).astype(np.int64)


E2M1 = np.array([0.0, 0.5, 1.0, 1.5, 2.0, 3.0, 4.0, 6.0, -0.0, -0.5, -1.0, -1.5, -2.0, -3.0, -4.0, -6.0])


def pack_weight(w, fmt):
    k, n = w.shape
    w = f64(np.asarray(w, np.float32).astype(ml_dtypes.bfloat16)).reshape(k // 32, 32, n)
    amax = np.abs(w).max(1)
    if fmt == "e4m3":
        byte = np.frexp(amax)[1] - 1 + 127 - 7
    else:
        mant, ex = np.frexp(amax / 6.0)
        byte = np.where(mant > 0.5, ex, ex - 1) + 127
    byte = np.clip(np.where(amax > 0, byte, 1), 1, 254)
    scaled = (w * np.exp2(127.0 - byte)[:, None, :]).reshape(k, n).astype(np.float32)
    by_word = np.ascontiguousarray(scaled.reshape(k // 512, 128, 4, n).transpose(0, 1, 3, 2))
    if fmt == "e4m3":
        words = by_word.astype(ml_dtypes.float8_e4m3fn).view(np.uint8)
    else:
        c = by_word.astype(ml_dtypes.float4_e2m1fn).view(np.uint8) & 0xF
        words = (c[..., 0::2] | (c[..., 1::2] << 4)).reshape(k // 512, 128, 2 * n)
    return np.ascontiguousarray(words), np.ascontiguousarray(byte.astype(np.uint8).reshape(k // 512, 16, n))


def unpack_weight(words, scales, fmt):
    g, _, n = scales.shape
    words = np.ascontiguousarray(words).reshape(g, 128, n, -1)
    if fmt == "e4m3":
        vals = words.view(ml_dtypes.float8_e4m3fn).astype(np.float64)
    else:
        nib = np.empty((g, 128, n, 4), np.uint8)
        nib[..., 0::2] = words & 0xF
        nib[..., 1::2] = words >> 4
        vals = E2M1[nib]
    vals = vals * np.repeat(np.exp2(scales.astype(np.float64) - 127.0), 8, axis=1)[..., None]
    return vals.transpose(0, 1, 3, 2).reshape(g * 512, n)


def gelu(v):
    return 0.5 * v * (1.0 + np.tanh(np.sqrt(2.0 / np.pi) * (v + 0.044715 * v**3)))


K, C, H, N, T, S = 1024, 512, 1024, 512, 2048, 1024

def setup_inputs():
    n = np.random.standard_normal
    s = mx_kscale(K)[:, None]
    s2 = mx_kscale(C)[:, None]
    u = mx_kscale(H)[:, None]
    tab_words, tab_scales = pack_weight(n((K, T)) * s, "e4m3")
    tab2_words, tab2_scales = pack_weight(n((C, T)) * s2, "e4m3")
    wb_words, wb_scales = pack_weight(n((C, H)) / np.sqrt(C) / s2, "e2m1")
    return {
        "tab_words": tab_words, "tab_scales": tab_scales,
        "tab2_words": tab2_words, "tab2_scales": tab2_scales,
        "offs": striped(np.random.permutation(T)[:S]),
        "offs2": striped(np.random.permutation(T)[:S]),
        "wa": (n((K, H)) / np.sqrt(K) / s).astype(np.float32),
        "wb_words": wb_words, "wb_scales": wb_scales,
        "eta": (np.exp(0.3 * n(H)) * u[:, 0]).astype(np.float32),
        "w": (2.0 * n((H, N)) / np.sqrt(H) / u).astype(np.float32),
        "gT": (0.8 * n((N, T))).astype(np.float32),
    }

def reference(tab_words, tab_scales, tab2_words, tab2_scales, offs, offs2, wa, wb_words, wb_scales, eta, w, gT):
    v = unpack_weight(tab_words, tab_scales, "e4m3")[:, unstriped(offs)]
    v2 = unpack_weight(tab2_words, tab2_scales, "e4m3")[:, unstriped(offs2)]
    wb = unpack_weight(wb_words, wb_scales, "e2m1")
    pre = np.tanh(mxq(f64(wa), 0, "e4m3").T @ v)
    post = np.tanh(wb.T @ v2)
    h = pre * post * f64(eta)[:, None]
    g = f64(gT)[:, unstriped(offs)]
    return g + (mxq(f64(w), 0, "e4m3").T @ mxq(h, 0, "e4m3"))

@@ -1,0 +1,305 @@
+from contextlib import ExitStack
+
+import concourse.mybir as mybir
+
+K, C, H, N, T, S = 1024, 512, 1024, 512, 2048, 1024
+FLOPS = 2 * S * (K * H + C * H + H * N)
+
+F32 = mybir.dt.float32
+BF16 = mybir.dt.bfloat16
+I32 = mybir.dt.int32
+U32 = mybir.dt.uint32
+U16 = mybir.dt.uint16
+U8 = mybir.dt.uint8
+FP8X4 = mybir.dt.float8_e4m3fn_x4
+FP4X4 = mybir.dt.float4_e2m1fn_x4
+ACT = mybir.ActivationFunctionType
+ALU = mybir.AluOpType
+
+P = 128
+PACK = 4
+PASS = P * PACK
+HALF = 512
+RUN = 4
+
+
+def tile_list_hebbian_trace_update_kernel(
+    tc, tab_words, tab_scales, tab2_words, tab2_scales, offs, offs2, wa, wb_words, wb_scales, eta, w, gT, out
+):
+    nc = tc.nc
+    with ExitStack() as ctx:
+        keep = ctx.enter_context(tc.tile_pool(name="keep", bufs=1))
+        raws = ctx.enter_context(tc.tile_pool(name="raws", bufs=4))
+        ring = ctx.enter_context(tc.tile_pool(name="ring", bufs=2))
+        ring4 = ctx.enter_context(tc.tile_pool(name="ring4", bufs=4))
+        psum = ctx.enter_context(tc.psum_pool(name="psum", bufs=8))
+
+        list1 = keep.tile([P, S // 16], U16, name="list1")
+        list2 = keep.tile([P, S // 16], U16, name="list2")
+        tab_w = [keep.tile([P, T], I32, name="tab_w%d" % a) for a in range(2)]
+        tab2_w = keep.tile([P, T], I32, name="tab2_w")
+        tab_s = keep.tile([P, T // 4], I32, name="tab_s")
+        tab2_s = keep.tile([P, T // 4], I32, name="tab2_s")
+        wb_w_raw = keep.tile([P, H // 2], I32, name="wb_w_raw")
+        wb_s_raw = keep.tile([P, H // 4], I32, name="wb_s_raw")
+        wb_w = keep.tile([P, H // 2], I32, name="wb_w", align_bytes=64)
+        wb_s = keep.tile([P, H // 4], I32, name="wb_s", align_bytes=64)
+        eta_sb = [[keep.tile([P, 1], F32, name="eta%d%d" % (b, t)) for t in range(PACK)] for b in range(2)]
+        g_tab = [keep.tile([P, T], F32, name="g_tab%d" % q) for q in range(4)]
+        warm = keep.tile([P, 8], F32, name="warm")
+        warm_out = keep.tile([P, 8], F32, name="warm_out")
+
+        nc.gpsimd.memset(tab_s[:], 0)
+        nc.vector.memset(warm[:], 0.0)
+        nc.scalar.activation(out=warm_out[:], in_=warm[:], func=ACT.Tanh)
+
+        wa_raw = {}
+        w_raw = {}
+
+        def load_wa(a, b):
+            raw = raws.tile([P, PACK, PASS], F32, name="raw")
+            rows = wa[a * PASS : (a + 1) * PASS, b * PASS : (b + 1) * PASS]
+            nc.sync.dma_start(out=raw[:], in_=rows.rearrange("(p j) c -> p j c", j=PACK))
+            wa_raw[(a, b)] = raw
+
+        def load_w(b):
+            raw = raws.tile([P, PACK, N], F32, name="raw")
+            rows = w[b * PASS : (b + 1) * PASS, :].rearrange("(m t i) n -> t m i n", t=PACK, i=RUN)
+            for t in range(PACK):
+                nc.sync.dma_start(out=raw[:, t, :], in_=rows[t])
+            w_raw[b] = raw
+
+        def load_words(dst, words):
+            nc.sync.dma_start(out=dst[:], in_=words.rearrange("p t i -> p (t i)").bitcast(I32))
+
+        def load_eta(b, t):
+            rates = eta[b * PASS : (b + 1) * PASS].rearrange("(m t i o) -> t m i o", t=PACK, i=RUN, o=1)
+            with nc.allow_non_contiguous_dma(reason="one learning rate to a partition"):
+                nc.sync.dma_start(out=eta_sb[b][t][:], in_=rates[t])
+
+        def load_g(q):
+            nc.sync.dma_start(out=g_tab[q][:], in_=gT[q * P : (q + 1) * P, :])
+
+        def load_plane(dst, rows):
+            for q in range(4):
+                quad = rows[4 * q : 4 * q + 4, :].bitcast(I32)
+                nc.sync.dma_start(
+                    out=dst[32 * q : 32 * (q + 1), :], in_=quad.unsqueeze(0).broadcast_to([8, 4, quad.shape[1]])
+                )
+
+        for q in range(4):
+            nc.gpsimd.dma_start(
+                out=tab_s[32 * q + 4 : 32 * q + 12, :], in_=tab_scales[:, 4 * q : 4 * q + 4, :].bitcast(I32)
+            )
+        nc.sync.dma_start(list2[:], offs2)
+        load_plane(tab2_s, tab2_scales[0])
+        nc.sync.dma_start(list1[:], offs)
+        load_words(tab2_w, tab2_words[0])
+        nc.sync.dma_start(out=wb_w_raw[:], in_=wb_words[0].bitcast(I32))
+        load_plane(wb_s_raw, wb_scales[0])
+        load_words(tab_w[0], tab_words[0])
+        load_wa(0, 0)
+        load_wa(1, 0)
+        load_words(tab_w[1], tab_words[1])
+        for t in range(PACK):
+            load_eta(0, t)
+        load_g(0)
+        load_wa(0, 1)
+        load_g(1)
+        load_wa(1, 1)
+        for t in range(PACK):
+            load_eta(1, t)
+        load_w(0)
+        load_g(2)
+        load_w(1)
+        load_g(3)
+
+        def gather(window, lst, jh, dtype, name):
+            dst = keep.tile([P, HALF], dtype, name=name, align_bytes=64)
+            cols = HALF // 16
+            nc.vector.tensor_copy(dst[:], window.indirect(lst[:, jh * cols : (jh + 1) * cols]))
+            return dst
+
+        v_w, v_s, v2_w, v2_s, g = {}, {}, {}, {}, {}
+
+        def gather_s2(jh):
+            v2_s[jh] = gather(tab2_s[:].bitcast(U8), list2, jh, U8, "v2_s%d" % jh)
+
+        def gather_s1(jh):
+            v_s[jh] = gather(tab_s[:].bitcast(U8), list1, jh, U8, "v_s%d" % jh)
+
+        def gather_w2(jh):
+            v2_w[jh] = gather(tab2_w[:].bitcast(U32), list2, jh, U32, "v2_w%d" % jh)
+
+        def gather_w1(a, jh):
+            v_w[(a, jh)] = gather(tab_w[a][:].bitcast(U32), list1, jh, U32, "v_w%d%d" % (a, jh))
+
+        def gather_g(q, jh):
+            g[(q, jh)] = gather(g_tab[q][:], list1, jh, F32, "g%d%d" % (q, jh))
+
+        def permute_wb():
+            nc.vector.tensor_copy(
+                out=wb_w[:].rearrange("p (t m e) -> p t m e", t=PACK, e=2),
+                in_=wb_w_raw[:].rearrange("p (m t e) -> p t m e", t=PACK, e=2),
+            )
+            nc.vector.tensor_copy(
+                out=wb_s[:].rearrange("p (t m) -> p t m", t=PACK),
+                in_=wb_s_raw[:].rearrange("p (m t) -> p t m", t=PACK),
+            )
+
+        def copy_on(engine, dst, src):
+            if engine == "scalar":
+                nc.scalar.copy(out=dst, in_=src)
+            else:
+                nc.vector.tensor_copy(out=dst, in_=src)
+
+        def quantize(grouped, name):
+            codes = keep.tile([P, PASS], U32, name=name + "_codes", align_bytes=64)
+            scales = keep.tile([P, PASS], U8, name=name + "_scales", align_bytes=64)
+            nc.vector.quantize_mx(out=codes[:].bitcast(FP8X4), scales=scales[:], in_=grouped[:])
+            return codes, scales
+
+        wa_g, wa_q, w_g, w_q = {}, {}, {}, {}
+
+        def cast_wa(a, b, engine):
+            grouped = ring.tile([P, PACK * PASS], BF16, name="grouped", align_bytes=64)
+            dst = grouped[:].rearrange("p (t m i j) -> p t m j i", t=PACK, i=RUN, j=PACK)
+            src = wa_raw[(a, b)][:].rearrange("p j (m t i) -> p t m j i", t=PACK, i=RUN)
+            for t in range(PACK):
+                copy_on(engine, dst[:, t], src[:, t])
+            wa_g[(a, b)] = grouped
+
+        def quant_wa(a, b):
+            wa_q[(a, b)] = quantize(wa_g[(a, b)], "wa%d%d" % (a, b))
+
+        def interleave(src, engine, name):
+            grouped = ring.tile([P, PACK * PASS], BF16, name=name, align_bytes=64)
+            copy_on(
+                engine,
+                grouped[:].rearrange("p (c i t) -> p c t i", t=PACK, i=RUN),
+                src[:].rearrange("p t (c i) -> p c t i", i=RUN),
+            )
+            return grouped
+
+        def cast_w(b, engine):
+            w_g[b] = interleave(w_raw[b], engine, "grouped")
+
+        def quant_w(b):
+            w_q[b] = quantize(w_g[b], "w%d" % b)
+
+        post, h_flat, h_g, h_q = {}, {}, {}, {}
+
+        def make_post(b, jh):
+            for t in range(PACK):
+                acc = psum.tile([P, HALF], F32, name="acc")
+                col = (2 * t + b) * P
+                nc.tensor.matmul_mx(
+                    out=acc[:],
+                    lhsT=wb_w[:].bitcast(U8)[:, 2 * col : 2 * (col + P)].bitcast(FP4X4),
+                    lhsT_scale=wb_s[:].bitcast(U8)[:, col : col + P],
+                    rhs=v2_w[jh][:].bitcast(FP8X4),
+                    rhs_scale=v2_s[jh][:],
+                    start=True,
+                    stop=True,
+                )
+                act = keep.tile([P, HALF], F32, name="post%d%d%d" % (b, jh, t))
+                nc.scalar.activation(out=act[:], in_=acc[:], func=ACT.Tanh)
+                post[(b, jh, t)] = act
+
+        def make_h(b, jh):
+            flat = ring.tile([P, PACK, HALF], BF16, name="flat")
+            for t in range(PACK):
+                acc = psum.tile([P, HALF], F32, name="acc")
+                for a in range(2):
+                    codes, scales = wa_q[(a, b)]
+                    nc.tensor.matmul_mx(
+                        out=acc[:],
+                        lhsT=codes[:, t * P : (t + 1) * P].bitcast(FP8X4),
+                        lhsT_scale=scales[:, t * P : (t + 1) * P],
+                        rhs=v_w[(a, jh)][:].bitcast(FP8X4),
+                        rhs_scale=v_s[jh][4 * (a + 1) : P, :],
+                        start=(a == 0),
+                        stop=(a == 1),
+                    )
+                pre = ring4.tile([P, HALF], F32, name="pre")
+                nc.scalar.activation(out=pre[:], in_=acc[:], func=ACT.Tanh)
+                nc.vector.scalar_tensor_tensor(
+                    out=flat[:, t, :],
+                    in0=pre[:],
+                    scalar=eta_sb[b][t][:],
+                    in1=post[(b, jh, t)][:],
+                    op0=ALU.mult,
+                    op1=ALU.mult,
+                )
+            h_flat[(b, jh)] = flat
+
+        def group_h(b, jh, engine):
+            h_g[(b, jh)] = interleave(h_flat[(b, jh)], engine, "h_grouped")
+
+        def quant_h(b, jh):
+            h_q[(b, jh)] = quantize(h_g[(b, jh)], "h%d%d" % (b, jh))
+
+        def finish(jh):
+            for q in range(4):
+                acc = psum.tile([P, HALF], F32, name="acc")
+                for b in range(2):
+                    w_codes, w_scales = w_q[b]
+                    h_codes, h_scales = h_q[(b, jh)]
+                    nc.tensor.matmul_mx(
+                        out=acc[:],
+                        lhsT=w_codes[:, q * P : (q + 1) * P].bitcast(FP8X4),
+                        lhsT_scale=w_scales[:, q * P : (q + 1) * P],
+                        rhs=h_codes[:].bitcast(FP8X4),
+                        rhs_scale=h_scales[:],
+                        start=(b == 0),
+                        stop=(b == 1),
+                    )
+                res = ring4.tile([P, HALF], F32, name="res")
+                nc.vector.tensor_tensor(out=res[:], in0=acc[:], in1=g[(q, jh)][:], op=ALU.add)
+                nc.sync.dma_start(out=out[q * P : (q + 1) * P, jh * HALF : (jh + 1) * HALF], in_=res[:])
+
+        gather_s2(0)
+        gather_w2(0)
+        permute_wb()
+        make_post(0, 0)
+        gather_s2(1)
+        gather_w2(1)
+        gather_w1(0, 0)
+        gather_s1(0)
+        cast_wa(0, 0, "scalar")
+        make_post(0, 1)
+        quant_wa(0, 0)
+        cast_wa(1, 0, "vector")
+        quant_wa(1, 0)
+        gather_w1(1, 0)
+        make_post(1, 0)
+        make_post(1, 1)
+        make_h(0, 0)
+        gather_s1(1)
+        gather_w1(0, 1)
+        gather_w1(1, 1)
+        make_h(0, 1)
+        cast_wa(0, 1, "scalar")
+        quant_wa(0, 1)
+        cast_wa(1, 1, "vector")
+        quant_wa(1, 1)
+        group_h(0, 0, "scalar")
+        make_h(1, 0)
+        group_h(0, 1, "scalar")
+        cast_w(0, "scalar")
+        make_h(1, 1)
+        group_h(1, 0, "vector")
+        cast_w(1, "scalar")
+        group_h(1, 1, "scalar")
+        quant_h(0, 0)
+        quant_w(0)
+        quant_h(0, 1)
+        quant_h(1, 0)
+        quant_w(1)
+        quant_h(1, 1)
+        for q in range(4):
+            gather_g(q, 0)
+        finish(0)
+        for q in range(4):
+            gather_g(q, 1)
+        finish(1)

@@ -21,6 +21,9 @@ PACK = 4
 PASS = P * PACK
 HALF = 512
 RUN = 4
+RES = ["wa00_codes","wa10_codes","wa01_codes","wa11_codes","wb_w_raw","tab2_s","tab_s","wb_w"]
+SHARE = {"w_raw0":"tab2_w","w_raw1":"tab_w1","w_grouped0":"wa_grouped00","w_grouped1":"wa_grouped10","h_grouped00":"wa_raw00","h_grouped01":"wa_raw10","h_grouped10":"wa_raw01","h_grouped11":"wa_raw11","flat10":"tab_w0"}
+WIDE = ["h0","gw10","gw11","gg2","gs2","gg0","gg1","gw2"]
 
 
 def tile_list_hebbian_trace_update_kernel(
@@ -29,122 +32,139 @@ def tile_list_hebbian_trace_update_kernel(
     nc = tc.nc
     with ExitStack() as ctx:
         keep = ctx.enter_context(tc.tile_pool(name="keep", bufs=1))
-        raws = ctx.enter_context(tc.tile_pool(name="raws", bufs=4))
-        ring = ctx.enter_context(tc.tile_pool(name="ring", bufs=2))
-        ring4 = ctx.enter_context(tc.tile_pool(name="ring4", bufs=4))
-        psum = ctx.enter_context(tc.psum_pool(name="psum", bufs=8))
+        psum = ctx.enter_context(tc.psum_pool(name="psum", bufs=1))
+        banks = []
+        pre_slots = []
+
+        def bank():
+            banks.append(psum.tile([P, HALF], F32, name="acc", tag="bank%d" % (len(banks) % 8)))
+            return banks[-1]
+
+        def pre_tile(width):
+            pre_slots.append(keep.tile([P, width], F32, name="pre", tag="pre%d" % (len(pre_slots) % 4)))
+            return pre_slots[-1]
+
+        def held(shape, dtype, name):
+            return keep.tile(shape, dtype, name=name, tag=SHARE.get(name, name), align_bytes=64)
+
+        def staged(name, ring_name, bufs):
+            return held([P, PACK * PASS], BF16, name)
 
         list1 = keep.tile([P, S // 16], U16, name="list1")
         list2 = keep.tile([P, S // 16], U16, name="list2")
-        tab_w = [keep.tile([P, T], I32, name="tab_w%d" % a) for a in range(2)]
-        tab2_w = keep.tile([P, T], I32, name="tab2_w")
-        tab_s = keep.tile([P, T // 4], I32, name="tab_s")
-        tab2_s = keep.tile([P, T // 4], I32, name="tab2_s")
-        wb_w_raw = keep.tile([P, H // 2], I32, name="wb_w_raw")
-        wb_s_raw = keep.tile([P, H // 4], I32, name="wb_s_raw")
-        wb_w = keep.tile([P, H // 2], I32, name="wb_w", align_bytes=64)
-        wb_s = keep.tile([P, H // 4], I32, name="wb_s", align_bytes=64)
-        eta_sb = [[keep.tile([P, 1], F32, name="eta%d%d" % (b, t)) for t in range(PACK)] for b in range(2)]
-        g_tab = [keep.tile([P, T], F32, name="g_tab%d" % q) for q in range(4)]
+        tab_w = [held([P, T], I32, "tab_w%d" % a) for a in range(2)]
+        tab2_w = held([P, T], I32, "tab2_w")
+        tab_s = held([P, T // 4], I32, "tab_s")
+        tab2_s = held([P, T // 4], I32, "tab2_s")
+        wb_w_raw = held([P, H // 2], I32, "wb_w_raw")
+        wb_s_raw = held([P, H // 4], I32, "wb_s_raw")
+        wb_w = held([P, H // 2], I32, "wb_w")
+        wb_s = held([P, H // 4], I32, "wb_s")
+        rates = keep.tile([P, 2, PACK], F32, name="rates")
+        eta_sb = [[rates[:, b, t : t + 1] for t in range(PACK)] for b in range(2)]
+        g_tab = [held([P, T], F32, "g_tab%d" % q) for q in range(4)]
         warm = keep.tile([P, 8], F32, name="warm")
         warm_out = keep.tile([P, 8], F32, name="warm_out")
 
-        nc.gpsimd.memset(tab_s[:], 0)
-        nc.vector.memset(warm[:], 0.0)
-        nc.scalar.activation(out=warm_out[:], in_=warm[:], func=ACT.Tanh)
+        nc.gpsimd.memset(tab2_s[:], 0)
+        nc.gpsimd.memset(warm[:], 0.0)
+        nc.vector.memset(tab_s[:], 0)
+        nc.vector.memset(wb_s_raw[:], 0)
 
         wa_raw = {}
         w_raw = {}
 
         def load_wa(a, b):
-            raw = raws.tile([P, PACK, PASS], F32, name="raw")
+            raw = held([P, PACK, PASS], F32, "wa_raw%d%d" % (a, b))
             rows = wa[a * PASS : (a + 1) * PASS, b * PASS : (b + 1) * PASS]
             nc.sync.dma_start(out=raw[:], in_=rows.rearrange("(p j) c -> p j c", j=PACK))
             wa_raw[(a, b)] = raw
 
         def load_w(b):
-            raw = raws.tile([P, PACK, N], F32, name="raw")
-            rows = w[b * PASS : (b + 1) * PASS, :].rearrange("(m t i) n -> t m i n", t=PACK, i=RUN)
-            for t in range(PACK):
-                nc.sync.dma_start(out=raw[:, t, :], in_=rows[t])
+            raw = held([P, PACK, N], F32, "w_raw%d" % b)
+            rows = w[b * PASS : (b + 1) * PASS, :]
+            nc.sync.dma_start(out=raw[:], in_=rows.rearrange("(p t) n -> p t n", t=PACK))
             w_raw[b] = raw
 
         def load_words(dst, words):
             nc.sync.dma_start(out=dst[:], in_=words.rearrange("p t i -> p (t i)").bitcast(I32))
 
-        def load_eta(b, t):
-            rates = eta[b * PASS : (b + 1) * PASS].rearrange("(m t i o) -> t m i o", t=PACK, i=RUN, o=1)
-            with nc.allow_non_contiguous_dma(reason="one learning rate to a partition"):
-                nc.sync.dma_start(out=eta_sb[b][t][:], in_=rates[t])
+        def load_eta():
+            nc.sync.dma_start(out=rates[:], in_=eta.rearrange("(b p t) -> p b t", b=2, t=PACK))
 
         def load_g(q):
             nc.sync.dma_start(out=g_tab[q][:], in_=gT[q * P : (q + 1) * P, :])
 
-        def load_plane(dst, rows):
+        def load_plane(queue, dst, rows):
             for q in range(4):
-                quad = rows[4 * q : 4 * q + 4, :].bitcast(I32)
+                queue.dma_start(out=dst[32 * q : 32 * q + 4, :], in_=rows[4 * q : 4 * q + 4, :].bitcast(I32))
+
+        def load_tab_planes():
+            for q in range(4):
                 nc.sync.dma_start(
-                    out=dst[32 * q : 32 * (q + 1), :], in_=quad.unsqueeze(0).broadcast_to([8, 4, quad.shape[1]])
+                    out=tab_s[32 * q + 4 : 32 * q + 12, :], in_=tab_scales[:, 4 * q : 4 * q + 4, :].bitcast(I32)
                 )
 
-        for q in range(4):
-            nc.gpsimd.dma_start(
-                out=tab_s[32 * q + 4 : 32 * q + 12, :], in_=tab_scales[:, 4 * q : 4 * q + 4, :].bitcast(I32)
-            )
-        nc.sync.dma_start(list2[:], offs2)
-        load_plane(tab2_s, tab2_scales[0])
-        nc.sync.dma_start(list1[:], offs)
-        load_words(tab2_w, tab2_words[0])
         nc.sync.dma_start(out=wb_w_raw[:], in_=wb_words[0].bitcast(I32))
-        load_plane(wb_s_raw, wb_scales[0])
+        nc.sync.dma_start(list2[:], offs2)
+        nc.sync.dma_start(list1[:], offs)
+        load_plane(nc.sync, tab2_s, tab2_scales[0])
+        load_words(tab2_w, tab2_words[0])
+        load_plane(nc.sync, wb_s_raw, wb_scales[0])
         load_words(tab_w[0], tab_words[0])
+        nc.scalar.activation(out=warm_out[:], in_=warm[:], func=ACT.Tanh)
+        load_words(tab_w[1], tab_words[1])
         load_wa(0, 0)
         load_wa(1, 0)
-        load_words(tab_w[1], tab_words[1])
-        for t in range(PACK):
-            load_eta(0, t)
+        load_tab_planes()
         load_g(0)
-        load_wa(0, 1)
-        load_g(1)
+        load_eta()
         load_wa(1, 1)
-        for t in range(PACK):
-            load_eta(1, t)
-        load_w(0)
+        load_wa(0, 1)
         load_g(2)
         load_w(1)
+        load_g(1)
+        load_w(0)
         load_g(3)
 
-        def gather(window, lst, jh, dtype, name):
-            dst = keep.tile([P, HALF], dtype, name=name, align_bytes=64)
+        def gather(store, key, wide_key, window, lst, jh, dtype, name):
             cols = HALF // 16
+            if wide_key in WIDE:
+                if key + (jh,) not in store:
+                    dst = held([P, S], dtype, name + "0")
+                    nc.vector.tensor_copy(dst[:], window.indirect(lst[:]))
+                    store[key + (0,)] = dst[:, 0:HALF]
+                    store[key + (1,)] = dst[:, HALF:S]
+                return
+            dst = held([P, HALF], dtype, name + "%d" % jh)
             nc.vector.tensor_copy(dst[:], window.indirect(lst[:, jh * cols : (jh + 1) * cols]))
-            return dst
+            store[key + (jh,)] = dst[:]
 
         v_w, v_s, v2_w, v2_s, g = {}, {}, {}, {}, {}
 
         def gather_s2(jh):
-            v2_s[jh] = gather(tab2_s[:].bitcast(U8), list2, jh, U8, "v2_s%d" % jh)
+            gather(v2_s, (), "gs2", tab2_s[:].bitcast(U8), list2, jh, U8, "v2_s")
 
         def gather_s1(jh):
-            v_s[jh] = gather(tab_s[:].bitcast(U8), list1, jh, U8, "v_s%d" % jh)
+            gather(v_s, (), "gs1", tab_s[:].bitcast(U8), list1, jh, U8, "v_s")
 
         def gather_w2(jh):
-            v2_w[jh] = gather(tab2_w[:].bitcast(U32), list2, jh, U32, "v2_w%d" % jh)
+            gather(v2_w, (), "gw2", tab2_w[:].bitcast(U32), list2, jh, U32, "v2_w")
 
         def gather_w1(a, jh):
-            v_w[(a, jh)] = gather(tab_w[a][:].bitcast(U32), list1, jh, U32, "v_w%d%d" % (a, jh))
+            gather(v_w, (a,), "gw1%d" % a, tab_w[a][:].bitcast(U32), list1, jh, U32, "v_w%d" % a)
 
         def gather_g(q, jh):
-            g[(q, jh)] = gather(g_tab[q][:], list1, jh, F32, "g%d%d" % (q, jh))
+            gather(g, (q,), "gg%d" % q, g_tab[q][:], list1, jh, F32, "g%d" % q)
 
         def permute_wb():
             nc.vector.tensor_copy(
-                out=wb_w[:].rearrange("p (t m e) -> p t m e", t=PACK, e=2),
-                in_=wb_w_raw[:].rearrange("p (m t e) -> p t m e", t=PACK, e=2),
+                out=wb_w[:].bitcast(U16).rearrange("p (t m) -> p t m", t=PACK),
+                in_=wb_w_raw[:].bitcast(U16).rearrange("p (m t) -> p t m", t=PACK),
             )
             nc.vector.tensor_copy(
-                out=wb_s[:].rearrange("p (t m) -> p t m", t=PACK),
-                in_=wb_s_raw[:].rearrange("p (m t) -> p t m", t=PACK),
+                out=wb_s[:].bitcast(U8).rearrange("p (t m) -> p t m", t=PACK),
+                in_=wb_s_raw[:].bitcast(U8).rearrange("p (m t) -> p t m", t=PACK),
             )
 
         def copy_on(engine, dst, src):
@@ -154,7 +174,7 @@ def tile_list_hebbian_trace_update_kernel(
                 nc.vector.tensor_copy(out=dst, in_=src)
 
         def quantize(grouped, name):
-            codes = keep.tile([P, PASS], U32, name=name + "_codes", align_bytes=64)
+            codes = held([P, PASS], U32, name + "_codes")
             scales = keep.tile([P, PASS], U8, name=name + "_scales", align_bytes=64)
             nc.vector.quantize_mx(out=codes[:].bitcast(FP8X4), scales=scales[:], in_=grouped[:])
             return codes, scales
@@ -162,27 +182,31 @@ def tile_list_hebbian_trace_update_kernel(
         wa_g, wa_q, w_g, w_q = {}, {}, {}, {}
 
         def cast_wa(a, b, engine):
-            grouped = ring.tile([P, PACK * PASS], BF16, name="grouped", align_bytes=64)
-            dst = grouped[:].rearrange("p (t m i j) -> p t m j i", t=PACK, i=RUN, j=PACK)
-            src = wa_raw[(a, b)][:].rearrange("p j (m t i) -> p t m j i", t=PACK, i=RUN)
-            for t in range(PACK):
-                copy_on(engine, dst[:, t], src[:, t])
+            grouped = staged("wa_grouped%d%d" % (a, b), "grouped", 3)
+            dst = grouped[:].rearrange("p (t m j) -> p m j t", t=PACK, j=PACK)
+            src = wa_raw[(a, b)][:].rearrange("p j (m t) -> p m j t", t=PACK)
+            copy_on(engine, dst, src)
             wa_g[(a, b)] = grouped
 
         def quant_wa(a, b):
             wa_q[(a, b)] = quantize(wa_g[(a, b)], "wa%d%d" % (a, b))
 
-        def interleave(src, engine, name):
-            grouped = ring.tile([P, PACK * PASS], BF16, name=name, align_bytes=64)
+        def interleave(src, engine, name, ring_name):
+            grouped = staged(name, ring_name, 3)
+            if engine == "gpsimd":
+                nc.gpsimd.tensor_scalar(
+                    grouped[:].rearrange("p (c t) -> p c t", t=PACK), src.rearrange("p t c -> p c t"), 1.0, 0.0, ALU.mult, ALU.add
+                )
+                return grouped
             copy_on(
                 engine,
                 grouped[:].rearrange("p (c i t) -> p c t i", t=PACK, i=RUN),
-                src[:].rearrange("p t (c i) -> p c t i", i=RUN),
+                src.rearrange("p t (c i) -> p c t i", i=RUN),
             )
             return grouped
 
         def cast_w(b, engine):
-            w_g[b] = interleave(w_raw[b], engine, "grouped")
+            w_g[b] = interleave(w_raw[b][:], engine, "w_grouped%d" % b, "grouped")
 
         def quant_w(b):
             w_q[b] = quantize(w_g[b], "w%d" % b)
@@ -191,57 +215,78 @@ def tile_list_hebbian_trace_update_kernel(
 
         def make_post(b, jh):
             for t in range(PACK):
-                acc = psum.tile([P, HALF], F32, name="acc")
+                acc = bank()
                 col = (2 * t + b) * P
                 nc.tensor.matmul_mx(
                     out=acc[:],
                     lhsT=wb_w[:].bitcast(U8)[:, 2 * col : 2 * (col + P)].bitcast(FP4X4),
                     lhsT_scale=wb_s[:].bitcast(U8)[:, col : col + P],
-                    rhs=v2_w[jh][:].bitcast(FP8X4),
-                    rhs_scale=v2_s[jh][:],
+                    rhs=v2_w[(jh,)].bitcast(FP8X4),
+                    rhs_scale=v2_s[(jh,)],
                     start=True,
                     stop=True,
                 )
-                act = keep.tile([P, HALF], F32, name="post%d%d%d" % (b, jh, t))
-                nc.scalar.activation(out=act[:], in_=acc[:], func=ACT.Tanh)
+                if "h%d" % b in WIDE:
+                    if (b, t) not in post:
+                        post[(b, t)] = held([P, S], F32, "post%d0%d" % (b, t))
+                    act = post[(b, t)][:, jh * HALF : (jh + 1) * HALF]
+                else:
+                    act = held([P, HALF], F32, "post%d%d%d" % (b, jh, t))[:]
+                nc.scalar.activation(out=act, in_=acc[:], func=ACT.Tanh)
                 post[(b, jh, t)] = act
 
-        def make_h(b, jh):
-            flat = ring.tile([P, PACK, HALF], BF16, name="flat")
-            for t in range(PACK):
-                acc = psum.tile([P, HALF], F32, name="acc")
-                for a in range(2):
-                    codes, scales = wa_q[(a, b)]
-                    nc.tensor.matmul_mx(
-                        out=acc[:],
-                        lhsT=codes[:, t * P : (t + 1) * P].bitcast(FP8X4),
-                        lhsT_scale=scales[:, t * P : (t + 1) * P],
-                        rhs=v_w[(a, jh)][:].bitcast(FP8X4),
-                        rhs_scale=v_s[jh][4 * (a + 1) : P, :],
-                        start=(a == 0),
-                        stop=(a == 1),
-                    )
-                pre = ring4.tile([P, HALF], F32, name="pre")
-                nc.scalar.activation(out=pre[:], in_=acc[:], func=ACT.Tanh)
-                nc.vector.scalar_tensor_tensor(
-                    out=flat[:, t, :],
-                    in0=pre[:],
-                    scalar=eta_sb[b][t][:],
-                    in1=post[(b, jh, t)][:],
-                    op0=ALU.mult,
-                    op1=ALU.mult,
+        def make_pre(b, jh, t, dst):
+            acc = bank()
+            for a in range(2):
+                codes, scales = wa_q[(a, b)]
+                nc.tensor.matmul_mx(
+                    out=acc[:],
+                    lhsT=codes[:, t * P : (t + 1) * P].bitcast(FP8X4),
+                    lhsT_scale=scales[:, t * P : (t + 1) * P],
+                    rhs=v_w[(a, jh)].bitcast(FP8X4),
+                    rhs_scale=v_s[(jh,)][4 * (a + 1) : P, :],
+                    start=(a == 0),
+                    stop=(a == 1),
                 )
-            h_flat[(b, jh)] = flat
+            nc.scalar.activation(out=dst, in_=acc[:], func=ACT.Tanh)
+
+        def product(dst, pre, rate, post_act):
+            nc.vector.scalar_tensor_tensor(
+                out=dst, in0=pre, scalar=rate, in1=post_act, op0=ALU.mult, op1=ALU.mult
+            )
+
+        seen = set()
+
+        def make_h(b, jh):
+            if "h%d" % b in WIDE:
+                if b not in seen:
+                    seen.add(b)
+                    return
+                flat = held([P, PACK, S], BF16, "flat%d" % b)
+                for t in range(PACK):
+                    pre = pre_tile(S)
+                    for j in range(2):
+                        make_pre(b, j, t, pre[:, j * HALF : (j + 1) * HALF])
+                    product(flat[:, t, :], pre[:], eta_sb[b][t], post[(b, t)][:])
+                for j in range(2):
+                    h_flat[(b, j)] = flat[:, :, j * HALF : (j + 1) * HALF]
+                return
+            flat = held([P, PACK, HALF], BF16, "flat%d%d" % (b, jh))
+            for t in range(PACK):
+                pre = pre_tile(HALF)
+                make_pre(b, jh, t, pre[:])
+                product(flat[:, t, :], pre[:], eta_sb[b][t], post[(b, jh, t)])
+            h_flat[(b, jh)] = flat[:]
 
         def group_h(b, jh, engine):
-            h_g[(b, jh)] = interleave(h_flat[(b, jh)], engine, "h_grouped")
+            h_g[(b, jh)] = interleave(h_flat[(b, jh)], engine, "h_grouped%d%d" % (b, jh), "h_grouped")
 
         def quant_h(b, jh):
             h_q[(b, jh)] = quantize(h_g[(b, jh)], "h%d%d" % (b, jh))
 
         def finish(jh):
             for q in range(4):
-                acc = psum.tile([P, HALF], F32, name="acc")
+                acc = bank()
                 for b in range(2):
                     w_codes, w_scales = w_q[b]
                     h_codes, h_scales = h_q[(b, jh)]
@@ -254,52 +299,56 @@ def tile_list_hebbian_trace_update_kernel(
                         start=(b == 0),
                         stop=(b == 1),
                     )
-                res = ring4.tile([P, HALF], F32, name="res")
-                nc.vector.tensor_tensor(out=res[:], in0=acc[:], in1=g[(q, jh)][:], op=ALU.add)
+                res = keep.tile([P, HALF], F32, name="res", tag=RES[4 * jh + q], align_bytes=64)
+                nc.vector.tensor_tensor(out=res[:], in0=acc[:], in1=g[(q, jh)], op=ALU.add)
                 nc.sync.dma_start(out=out[q * P : (q + 1) * P, jh * HALF : (jh + 1) * HALF], in_=res[:])
 
-        gather_s2(0)
-        gather_w2(0)
-        permute_wb()
-        make_post(0, 0)
-        gather_s2(1)
-        gather_w2(1)
-        gather_w1(0, 0)
+        gather_w1(1, 1)
+        gather_g(1, 1)
         gather_s1(0)
-        cast_wa(0, 0, "scalar")
-        make_post(0, 1)
-        quant_wa(0, 0)
+        cast_wa(0, 1, "scalar")
+        gather_s2(1)
+        gather_g(2, 0)
+        cast_wa(0, 0, "vector")
+        gather_w2(1)
+        permute_wb()
         cast_wa(1, 0, "vector")
         quant_wa(1, 0)
-        gather_w1(1, 0)
-        make_post(1, 0)
-        make_post(1, 1)
-        make_h(0, 0)
-        gather_s1(1)
-        gather_w1(0, 1)
-        gather_w1(1, 1)
-        make_h(0, 1)
-        cast_wa(0, 1, "scalar")
-        quant_wa(0, 1)
+        gather_s2(0)
+        quant_wa(0, 0)
         cast_wa(1, 1, "vector")
-        quant_wa(1, 1)
-        group_h(0, 0, "scalar")
-        make_h(1, 0)
-        group_h(0, 1, "scalar")
-        cast_w(0, "scalar")
-        make_h(1, 1)
-        group_h(1, 0, "vector")
+        gather_w1(1, 0)
+        gather_w2(0)
         cast_w(1, "scalar")
-        group_h(1, 1, "scalar")
-        quant_h(0, 0)
-        quant_w(0)
-        quant_h(0, 1)
-        quant_h(1, 0)
+        quant_wa(1, 1)
+        gather_g(2, 1)
+        make_post(0, 1)
+        gather_s1(1)
+        quant_wa(0, 1)
+        make_post(1, 1)
+        gather_w1(0, 1)
+        make_h(1, 1)
+        make_h(0, 1)
         quant_w(1)
+        gather_g(3, 1)
+        gather_w1(0, 0)
+        make_post(1, 0)
+        gather_g(0, 1)
+        make_post(0, 0)
+        make_h(1, 0)
+        make_h(0, 0)
+        cast_w(0, "vector")
+        group_h(1, 1, "scalar")
+        quant_w(0)
+        gather_g(0, 0)
+        group_h(0, 1, "scalar")
+        quant_h(0, 1)
+        group_h(1, 0, "scalar")
+        gather_g(1, 0)
         quant_h(1, 1)
-        for q in range(4):
-            gather_g(q, 0)
-        finish(0)
-        for q in range(4):
-            gather_g(q, 1)
+        group_h(0, 0, "scalar")
+        gather_g(3, 0)
+        quant_h(1, 0)
+        quant_h(0, 0)
         finish(1)
+        finish(0)

@@ -13,17 +13,20 @@ U16 = mybir.dt.uint16
 U8 = mybir.dt.uint8
 FP8X4 = mybir.dt.float8_e4m3fn_x4
 FP4X4 = mybir.dt.float4_e2m1fn_x4
-ACT = mybir.ActivationFunctionType
-ALU = mybir.AluOpType
+TANH = mybir.ActivationFunctionType.Tanh
+MULT = mybir.AluOpType.mult
+ADD = mybir.AluOpType.add
 
 P = 128
-PACK = 4
-PASS = P * PACK
-HALF = 512
+SLOTS = 4
+PASS = P * SLOTS
+QUADRANT = 32
+LIST_ROWS = 16
+HALF = S // 2
+QUARTER = HALF // 2
 RUN = 4
-RES = ["wa00_codes","wa10_codes","wa01_codes","wa11_codes","wb_w_raw","tab2_s","tab_s","wb_w"]
-SHARE = {"w_raw0":"tab2_w","w_raw1":"tab_w1","w_grouped0":"wa_grouped00","w_grouped1":"wa_grouped10","h_grouped00":"wa_raw00","h_grouped01":"wa_raw10","h_grouped10":"wa_raw01","h_grouped11":"wa_raw11","flat10":"tab_w0"}
-WIDE = ["h0","gw10","gw11","gg2","gs2","gg0","gg1","gw2"]
+BANKS = 8
+PRE_SLOTS = 4
 
 
 def tile_list_hebbian_trace_update_kernel(
@@ -31,27 +34,28 @@ def tile_list_hebbian_trace_update_kernel(
 ):
     nc = tc.nc
     with ExitStack() as ctx:
-        keep = ctx.enter_context(tc.tile_pool(name="keep", bufs=1))
+        sbuf = ctx.enter_context(tc.tile_pool(name="sbuf", bufs=1))
         psum = ctx.enter_context(tc.psum_pool(name="psum", bufs=1))
-        banks = []
-        pre_slots = []
 
-        def bank():
-            banks.append(psum.tile([P, HALF], F32, name="acc", tag="bank%d" % (len(banks) % 8)))
+        tags = {}
+
+        def held(shape, dtype, name, after=None):
+            tags[name] = tags[after] if after else name
+            return sbuf.tile(shape, dtype, name=name, tag=tags[name], align_bytes=64)
+
+        banks = []
+        pre_tiles = []
+
+        def next_bank():
+            banks.append(psum.tile([P, HALF], F32, name="acc", tag="bank%d" % (len(banks) % BANKS)))
             return banks[-1]
 
-        def pre_tile(width):
-            pre_slots.append(keep.tile([P, width], F32, name="pre", tag="pre%d" % (len(pre_slots) % 4)))
-            return pre_slots[-1]
+        def next_pre():
+            pre_tiles.append(sbuf.tile([P, S], F32, name="pre", tag="pre%d" % (len(pre_tiles) % PRE_SLOTS)))
+            return pre_tiles[-1]
 
-        def held(shape, dtype, name):
-            return keep.tile(shape, dtype, name=name, tag=SHARE.get(name, name), align_bytes=64)
-
-        def staged(name, ring_name, bufs):
-            return held([P, PACK * PASS], BF16, name)
-
-        list1 = keep.tile([P, S // 16], U16, name="list1")
-        list2 = keep.tile([P, S // 16], U16, name="list2")
+        list1 = sbuf.tile([P, S // LIST_ROWS], U16, name="list1")
+        list2 = sbuf.tile([P, S // LIST_ROWS], U16, name="list2")
         tab_w = [held([P, T], I32, "tab_w%d" % a) for a in range(2)]
         tab2_w = held([P, T], I32, "tab2_w")
         tab_s = held([P, T // 4], I32, "tab_s")
@@ -60,295 +64,226 @@ def tile_list_hebbian_trace_update_kernel(
         wb_s_raw = held([P, H // 4], I32, "wb_s_raw")
         wb_w = held([P, H // 2], I32, "wb_w")
         wb_s = held([P, H // 4], I32, "wb_s")
-        rates = keep.tile([P, 2, PACK], F32, name="rates")
-        eta_sb = [[rates[:, b, t : t + 1] for t in range(PACK)] for b in range(2)]
-        g_tab = [held([P, T], F32, "g_tab%d" % q) for q in range(4)]
-        warm = keep.tile([P, 8], F32, name="warm")
-        warm_out = keep.tile([P, 8], F32, name="warm_out")
+        rates = sbuf.tile([P, 2, SLOTS], F32, name="rates")
+        g_tab = [held([P, T], F32, "g_tab%d" % q) for q in range(N // P)]
 
         nc.gpsimd.memset(tab2_s[:], 0)
-        nc.gpsimd.memset(warm[:], 0.0)
         nc.vector.memset(tab_s[:], 0)
         nc.vector.memset(wb_s_raw[:], 0)
 
-        wa_raw = {}
-        w_raw = {}
+        wa_raw, w_raw = {}, {}
 
         def load_wa(a, b):
-            raw = held([P, PACK, PASS], F32, "wa_raw%d%d" % (a, b))
+            wa_raw[(a, b)] = held([P, SLOTS, PASS], F32, "wa_raw%d%d" % (a, b))
             rows = wa[a * PASS : (a + 1) * PASS, b * PASS : (b + 1) * PASS]
-            nc.sync.dma_start(out=raw[:], in_=rows.rearrange("(p j) c -> p j c", j=PACK))
-            wa_raw[(a, b)] = raw
+            nc.sync.dma_start(out=wa_raw[(a, b)][:], in_=rows.rearrange("(p j) c -> p j c", j=SLOTS))
 
-        def load_w(b):
-            raw = held([P, PACK, N], F32, "w_raw%d" % b)
+        def load_w(b, after):
+            w_raw[b] = held([P, SLOTS, N], F32, "w_raw%d" % b, after)
             rows = w[b * PASS : (b + 1) * PASS, :]
-            nc.sync.dma_start(out=raw[:], in_=rows.rearrange("(p t) n -> p t n", t=PACK))
-            w_raw[b] = raw
+            nc.sync.dma_start(out=w_raw[b][:], in_=rows.rearrange("(p t) n -> p t n", t=SLOTS))
 
         def load_words(dst, words):
             nc.sync.dma_start(out=dst[:], in_=words.rearrange("p t i -> p (t i)").bitcast(I32))
 
-        def load_eta():
-            nc.sync.dma_start(out=rates[:], in_=eta.rearrange("(b p t) -> p b t", b=2, t=PACK))
-
         def load_g(q):
             nc.sync.dma_start(out=g_tab[q][:], in_=gT[q * P : (q + 1) * P, :])
 
-        def load_plane(queue, dst, rows):
-            for q in range(4):
-                queue.dma_start(out=dst[32 * q : 32 * q + 4, :], in_=rows[4 * q : 4 * q + 4, :].bitcast(I32))
+        def load_plane(dst, rows):
+            for u in range(P // QUADRANT):
+                first = QUADRANT * u
+                nc.sync.dma_start(out=dst[first : first + 4, :], in_=rows[4 * u : 4 * u + 4, :].bitcast(I32))
 
         def load_tab_planes():
-            for q in range(4):
+            for u in range(P // QUADRANT):
+                first = QUADRANT * u + 4
                 nc.sync.dma_start(
-                    out=tab_s[32 * q + 4 : 32 * q + 12, :], in_=tab_scales[:, 4 * q : 4 * q + 4, :].bitcast(I32)
+                    out=tab_s[first : first + 8, :], in_=tab_scales[:, 4 * u : 4 * u + 4, :].bitcast(I32)
                 )
 
         nc.sync.dma_start(out=wb_w_raw[:], in_=wb_words[0].bitcast(I32))
         nc.sync.dma_start(list2[:], offs2)
-        nc.sync.dma_start(list1[:], offs)
-        load_plane(nc.sync, tab2_s, tab2_scales[0])
+        load_plane(tab2_s, tab2_scales[0])
         load_words(tab2_w, tab2_words[0])
-        load_plane(nc.sync, wb_s_raw, wb_scales[0])
+        load_plane(wb_s_raw, wb_scales[0])
+        nc.sync.dma_start(list1[:], offs)
         load_words(tab_w[0], tab_words[0])
-        nc.scalar.activation(out=warm_out[:], in_=warm[:], func=ACT.Tanh)
-        load_words(tab_w[1], tab_words[1])
         load_wa(0, 0)
         load_wa(1, 0)
         load_tab_planes()
-        load_g(0)
-        load_eta()
+        load_words(tab_w[1], tab_words[1])
         load_wa(1, 1)
         load_wa(0, 1)
-        load_g(2)
-        load_w(1)
+        nc.sync.dma_start(out=rates[:], in_=eta.rearrange("(b p t) -> p b t", b=2, t=SLOTS))
+        load_g(0)
+        load_w(0, after="tab2_w")
         load_g(1)
-        load_w(0)
+        load_w(1, after="tab_w0")
+        load_g(2)
         load_g(3)
 
-        def gather(store, key, wide_key, window, lst, jh, dtype, name):
-            cols = HALF // 16
-            if wide_key in WIDE:
-                if key + (jh,) not in store:
-                    dst = held([P, S], dtype, name + "0")
-                    nc.vector.tensor_copy(dst[:], window.indirect(lst[:]))
-                    store[key + (0,)] = dst[:, 0:HALF]
-                    store[key + (1,)] = dst[:, HALF:S]
-                return
-            dst = held([P, HALF], dtype, name + "%d" % jh)
-            nc.vector.tensor_copy(dst[:], window.indirect(lst[:, jh * cols : (jh + 1) * cols]))
-            store[key + (jh,)] = dst[:]
+        def halves(tile):
+            return [tile[:, 0:HALF], tile[:, HALF:S]]
 
-        v_w, v_s, v2_w, v2_s, g = {}, {}, {}, {}, {}
-
-        def gather_s2(jh):
-            gather(v2_s, (), "gs2", tab2_s[:].bitcast(U8), list2, jh, U8, "v2_s")
-
-        def gather_s1(jh):
-            gather(v_s, (), "gs1", tab_s[:].bitcast(U8), list1, jh, U8, "v_s")
-
-        def gather_w2(jh):
-            gather(v2_w, (), "gw2", tab2_w[:].bitcast(U32), list2, jh, U32, "v2_w")
-
-        def gather_w1(a, jh):
-            gather(v_w, (a,), "gw1%d" % a, tab_w[a][:].bitcast(U32), list1, jh, U32, "v_w%d" % a)
-
-        def gather_g(q, jh):
-            gather(g, (q,), "gg%d" % q, g_tab[q][:], list1, jh, F32, "g%d" % q)
-
-        def permute_wb():
-            nc.vector.tensor_copy(
-                out=wb_w[:].bitcast(U16).rearrange("p (t m) -> p t m", t=PACK),
-                in_=wb_w_raw[:].bitcast(U16).rearrange("p (m t) -> p t m", t=PACK),
-            )
-            nc.vector.tensor_copy(
-                out=wb_s[:].bitcast(U8).rearrange("p (t m) -> p t m", t=PACK),
-                in_=wb_s_raw[:].bitcast(U8).rearrange("p (m t) -> p t m", t=PACK),
-            )
-
-        def copy_on(engine, dst, src):
-            if engine == "scalar":
-                nc.scalar.copy(out=dst, in_=src)
-            else:
-                nc.vector.tensor_copy(out=dst, in_=src)
+        def gather(window, offsets, dtype, name, after=None):
+            picked = held([P, offsets.shape[1] * LIST_ROWS], dtype, name, after)
+            nc.vector.tensor_copy(picked[:], window.indirect(offsets))
+            return picked
 
         def quantize(grouped, name):
             codes = held([P, PASS], U32, name + "_codes")
-            scales = keep.tile([P, PASS], U8, name=name + "_scales", align_bytes=64)
+            scales = held([P, PASS], U8, name + "_scales")
             nc.vector.quantize_mx(out=codes[:].bitcast(FP8X4), scales=scales[:], in_=grouped[:])
             return codes, scales
 
-        wa_g, wa_q, w_g, w_q = {}, {}, {}, {}
-
-        def cast_wa(a, b, engine):
-            grouped = staged("wa_grouped%d%d" % (a, b), "grouped", 3)
-            dst = grouped[:].rearrange("p (t m j) -> p m j t", t=PACK, j=PACK)
-            src = wa_raw[(a, b)][:].rearrange("p j (m t) -> p m j t", t=PACK)
-            copy_on(engine, dst, src)
-            wa_g[(a, b)] = grouped
-
-        def quant_wa(a, b):
-            wa_q[(a, b)] = quantize(wa_g[(a, b)], "wa%d%d" % (a, b))
-
-        def interleave(src, engine, name, ring_name):
-            grouped = staged(name, ring_name, 3)
-            if engine == "gpsimd":
-                nc.gpsimd.tensor_scalar(
-                    grouped[:].rearrange("p (c t) -> p c t", t=PACK), src.rearrange("p t c -> p c t"), 1.0, 0.0, ALU.mult, ALU.add
-                )
-                return grouped
-            copy_on(
-                engine,
-                grouped[:].rearrange("p (c i t) -> p c t i", t=PACK, i=RUN),
-                src.rearrange("p t (c i) -> p c t i", i=RUN),
+        def quantize_wa(a, b):
+            grouped = held([P, SLOTS * PASS], BF16, "wa_grouped%d%d" % (a, b))
+            nc.vector.tensor_copy(
+                out=grouped[:].rearrange("p (t m j) -> p m j t", t=SLOTS, j=SLOTS),
+                in_=wa_raw[(a, b)][:].rearrange("p j (m t) -> p m j t", t=SLOTS),
             )
+            return quantize(grouped, "wa%d%d" % (a, b))
+
+        def interleave(rows, name, after=None, pieces=1):
+            grouped = held([P, SLOTS * PASS], BF16, name, after)
+            dst = grouped[:].rearrange("p (c i t) -> p c t i", t=SLOTS, i=RUN)
+            src = rows.rearrange("p t (c i) -> p c t i", i=RUN)
+            step = PASS // RUN // pieces
+            for u in range(pieces):
+                nc.scalar.copy(out=dst[:, u * step : (u + 1) * step], in_=src[:, u * step : (u + 1) * step])
             return grouped
 
-        def cast_w(b, engine):
-            w_g[b] = interleave(w_raw[b][:], engine, "w_grouped%d" % b, "grouped")
+        v2_s = halves(gather(tab2_s[:].bitcast(U8), list2[:], U8, "v2_s"))
+        v2_w = halves(gather(tab2_w[:].bitcast(U32), list2[:], U32, "v2_w"))
+        nc.vector.tensor_copy(
+            out=wb_w[:].bitcast(U16).rearrange("p (t m) -> p t m", t=SLOTS),
+            in_=wb_w_raw[:].bitcast(U16).rearrange("p (m t) -> p t m", t=SLOTS),
+        )
+        nc.vector.tensor_copy(
+            out=wb_s[:].bitcast(U8).rearrange("p (t m) -> p t m", t=SLOTS),
+            in_=wb_s_raw[:].bitcast(U8).rearrange("p (m t) -> p t m", t=SLOTS),
+        )
 
-        def quant_w(b):
-            w_q[b] = quantize(w_g[b], "w%d" % b)
+        wa_q = {}
+        v_w = [halves(gather(tab_w[0][:].bitcast(U32), list1[:], U32, "v_w0"))]
+        wa_q[(0, 0)] = quantize_wa(0, 0)
+        wa_q[(1, 0)] = quantize_wa(1, 0)
+        v_s = halves(gather(tab_s[:].bitcast(U8), list1[:], U8, "v_s"))
+        half_cols = HALF // LIST_ROWS
+        v_w.append(
+            [
+                gather(
+                    tab_w[1][:].bitcast(U32), list1[:, jh * half_cols : (jh + 1) * half_cols], U32, "v_w1%d" % jh
+                )[:]
+                for jh in range(2)
+            ]
+        )
+        wa_q[(1, 1)] = quantize_wa(1, 1)
+        wa_q[(0, 1)] = quantize_wa(0, 1)
 
-        post, h_flat, h_g, h_q = {}, {}, {}, {}
+        post = {}
+        for b in range(2):
+            for jh in range(2):
+                for t in range(SLOTS):
+                    acc = next_bank()
+                    col = (2 * t + b) * P
+                    nc.tensor.matmul_mx(
+                        out=acc[:],
+                        lhsT=wb_w[:].bitcast(U8)[:, 2 * col : 2 * (col + P)].bitcast(FP4X4),
+                        lhsT_scale=wb_s[:].bitcast(U8)[:, col : col + P],
+                        rhs=v2_w[jh].bitcast(FP8X4),
+                        rhs_scale=v2_s[jh],
+                        start=True,
+                        stop=True,
+                    )
+                    if jh == 0:
+                        post[(b, t)] = held([P, S], F32, "post%d%d" % (b, t))
+                    nc.scalar.activation(out=halves(post[(b, t)])[jh], in_=acc[:], func=TANH)
 
-        def make_post(b, jh):
-            for t in range(PACK):
-                acc = bank()
-                col = (2 * t + b) * P
-                nc.tensor.matmul_mx(
-                    out=acc[:],
-                    lhsT=wb_w[:].bitcast(U8)[:, 2 * col : 2 * (col + P)].bitcast(FP4X4),
-                    lhsT_scale=wb_s[:].bitcast(U8)[:, col : col + P],
-                    rhs=v2_w[(jh,)].bitcast(FP8X4),
-                    rhs_scale=v2_s[(jh,)],
-                    start=True,
-                    stop=True,
+        def make_h(b, after):
+            flat = held([P, SLOTS, S], BF16, "flat%d" % b, after)
+            for t in range(SLOTS):
+                pre = next_pre()
+                for jh in range(2):
+                    acc = next_bank()
+                    for a in range(2):
+                        codes, scales = wa_q[(a, b)]
+                        nc.tensor.matmul_mx(
+                            out=acc[:],
+                            lhsT=codes[:, t * P : (t + 1) * P].bitcast(FP8X4),
+                            lhsT_scale=scales[:, t * P : (t + 1) * P],
+                            rhs=v_w[a][jh].bitcast(FP8X4),
+                            rhs_scale=v_s[jh][4 * (a + 1) : P, :],
+                            start=(a == 0),
+                            stop=(a == 1),
+                        )
+                    nc.scalar.activation(out=halves(pre)[jh], in_=acc[:], func=TANH)
+                nc.vector.scalar_tensor_tensor(
+                    out=flat[:, t, :],
+                    in0=pre[:],
+                    scalar=rates[:, b, t : t + 1],
+                    in1=post[(b, t)][:],
+                    op0=MULT,
+                    op1=MULT,
                 )
-                if "h%d" % b in WIDE:
-                    if (b, t) not in post:
-                        post[(b, t)] = held([P, S], F32, "post%d0%d" % (b, t))
-                    act = post[(b, t)][:, jh * HALF : (jh + 1) * HALF]
-                else:
-                    act = held([P, HALF], F32, "post%d%d%d" % (b, jh, t))[:]
-                nc.scalar.activation(out=act, in_=acc[:], func=ACT.Tanh)
-                post[(b, jh, t)] = act
+            return [flat[:, :, 0:HALF], flat[:, :, HALF:S]]
 
-        def make_pre(b, jh, t, dst):
-            acc = bank()
-            for a in range(2):
-                codes, scales = wa_q[(a, b)]
-                nc.tensor.matmul_mx(
-                    out=acc[:],
-                    lhsT=codes[:, t * P : (t + 1) * P].bitcast(FP8X4),
-                    lhsT_scale=scales[:, t * P : (t + 1) * P],
-                    rhs=v_w[(a, jh)].bitcast(FP8X4),
-                    rhs_scale=v_s[(jh,)][4 * (a + 1) : P, :],
-                    start=(a == 0),
-                    stop=(a == 1),
-                )
-            nc.scalar.activation(out=dst, in_=acc[:], func=ACT.Tanh)
+        def gather_g(q, after=None):
+            return halves(gather(g_tab[q][:], list1[:], F32, "g%d" % q, after))
 
-        def product(dst, pre, rate, post_act):
-            nc.vector.scalar_tensor_tensor(
-                out=dst, in0=pre, scalar=rate, in1=post_act, op0=ALU.mult, op1=ALU.mult
+        g = {}
+        h_flat = [make_h(0, after="wa_raw00")]
+        g[0] = gather_g(0)
+        h_flat.append(make_h(1, after="g_tab0"))
+
+        h_grouped, w_grouped = {}, {}
+        h_grouped[(0, 0)] = interleave(h_flat[0][0], "h_grouped00", after="wa_grouped00")
+        w_grouped[0] = interleave(w_raw[0][:], "w_grouped0", after="wa01_codes")
+        w_grouped[1] = interleave(w_raw[1][:], "w_grouped1")
+        h_grouped[(1, 0)] = interleave(h_flat[1][0], "h_grouped10", after="wa_grouped11")
+        h_grouped[(0, 1)] = interleave(h_flat[0][1], "h_grouped01", after="w_raw1")
+        h_grouped[(1, 1)] = interleave(h_flat[1][1], "h_grouped11", after="wa_grouped01", pieces=2)
+
+        h_q, w_q = {}, {}
+        g[1] = gather_g(1)
+        h_q[(0, 0)] = quantize(h_grouped[(0, 0)], "h00")
+        w_q[0] = quantize(w_grouped[0], "w0")
+        g[2] = gather_g(2)
+        w_q[1] = quantize(w_grouped[1], "w1")
+        h_q[(1, 0)] = quantize(h_grouped[(1, 0)], "h10")
+        g[3] = gather_g(3, after="h_grouped10")
+        h_q[(0, 1)] = quantize(h_grouped[(0, 1)], "h01")
+        last_codes = held([P, PASS], U32, "h11_codes")
+        last_scales = held([P, PASS], U8, "h11_scales")
+        for lo in (0, QUARTER):
+            nc.vector.quantize_mx(
+                out=last_codes[:, lo : lo + QUARTER].bitcast(FP8X4),
+                scales=last_scales[:, lo : lo + QUARTER],
+                in_=h_grouped[(1, 1)][:, SLOTS * lo : SLOTS * (lo + QUARTER)],
             )
+        h_q[(1, 1)] = (last_codes, last_scales)
 
-        seen = set()
-
-        def make_h(b, jh):
-            if "h%d" % b in WIDE:
-                if b not in seen:
-                    seen.add(b)
-                    return
-                flat = held([P, PACK, S], BF16, "flat%d" % b)
-                for t in range(PACK):
-                    pre = pre_tile(S)
-                    for j in range(2):
-                        make_pre(b, j, t, pre[:, j * HALF : (j + 1) * HALF])
-                    product(flat[:, t, :], pre[:], eta_sb[b][t], post[(b, t)][:])
-                for j in range(2):
-                    h_flat[(b, j)] = flat[:, :, j * HALF : (j + 1) * HALF]
-                return
-            flat = held([P, PACK, HALF], BF16, "flat%d%d" % (b, jh))
-            for t in range(PACK):
-                pre = pre_tile(HALF)
-                make_pre(b, jh, t, pre[:])
-                product(flat[:, t, :], pre[:], eta_sb[b][t], post[(b, jh, t)])
-            h_flat[(b, jh)] = flat[:]
-
-        def group_h(b, jh, engine):
-            h_g[(b, jh)] = interleave(h_flat[(b, jh)], engine, "h_grouped%d%d" % (b, jh), "h_grouped")
-
-        def quant_h(b, jh):
-            h_q[(b, jh)] = quantize(h_g[(b, jh)], "h%d%d" % (b, jh))
-
-        def finish(jh):
-            for q in range(4):
-                acc = bank()
+        def finish(jh, lo, width, spent):
+            cols = slice(lo, lo + width)
+            for q in range(N // P):
+                acc = next_bank()
                 for b in range(2):
                     w_codes, w_scales = w_q[b]
                     h_codes, h_scales = h_q[(b, jh)]
                     nc.tensor.matmul_mx(
-                        out=acc[:],
+                        out=acc[:, 0:width],
                         lhsT=w_codes[:, q * P : (q + 1) * P].bitcast(FP8X4),
                         lhsT_scale=w_scales[:, q * P : (q + 1) * P],
-                        rhs=h_codes[:].bitcast(FP8X4),
-                        rhs_scale=h_scales[:],
+                        rhs=h_codes[:, cols].bitcast(FP8X4),
+                        rhs_scale=h_scales[:, cols],
                         start=(b == 0),
                         stop=(b == 1),
                     )
-                res = keep.tile([P, HALF], F32, name="res", tag=RES[4 * jh + q], align_bytes=64)
-                nc.vector.tensor_tensor(out=res[:], in0=acc[:], in1=g[(q, jh)], op=ALU.add)
-                nc.sync.dma_start(out=out[q * P : (q + 1) * P, jh * HALF : (jh + 1) * HALF], in_=res[:])
+                first = jh * HALF + lo
+                res = held([P, width], F32, "res%d_%d" % (q, first), spent[q])
+                nc.vector.tensor_tensor(out=res[:], in0=acc[:, 0:width], in1=g[q][jh][:, cols], op=ADD)
+                nc.sync.dma_start(out=out[q * P : (q + 1) * P, first : first + width], in_=res[:])
 
-        gather_w1(1, 1)
-        gather_g(1, 1)
-        gather_s1(0)
-        cast_wa(0, 1, "scalar")
-        gather_s2(1)
-        gather_g(2, 0)
-        cast_wa(0, 0, "vector")
-        gather_w2(1)
-        permute_wb()
-        cast_wa(1, 0, "vector")
-        quant_wa(1, 0)
-        gather_s2(0)
-        quant_wa(0, 0)
-        cast_wa(1, 1, "vector")
-        gather_w1(1, 0)
-        gather_w2(0)
-        cast_w(1, "scalar")
-        quant_wa(1, 1)
-        gather_g(2, 1)
-        make_post(0, 1)
-        gather_s1(1)
-        quant_wa(0, 1)
-        make_post(1, 1)
-        gather_w1(0, 1)
-        make_h(1, 1)
-        make_h(0, 1)
-        quant_w(1)
-        gather_g(3, 1)
-        gather_w1(0, 0)
-        make_post(1, 0)
-        gather_g(0, 1)
-        make_post(0, 0)
-        make_h(1, 0)
-        make_h(0, 0)
-        cast_w(0, "vector")
-        group_h(1, 1, "scalar")
-        quant_w(0)
-        gather_g(0, 0)
-        group_h(0, 1, "scalar")
-        quant_h(0, 1)
-        group_h(1, 0, "scalar")
-        gather_g(1, 0)
-        quant_h(1, 1)
-        group_h(0, 0, "scalar")
-        gather_g(3, 0)
-        quant_h(1, 0)
-        quant_h(0, 0)
-        finish(1)
-        finish(0)
+        finish(0, 0, HALF, spent=["wa00_codes", "wa10_codes", "wb_w", "wa11_codes"])
+        finish(1, 0, QUARTER, spent=[None] * (N // P))
+        finish(1, QUARTER, QUARTER, spent=[None] * (N // P))

@@ -23,10 +23,9 @@ PASS = P * SLOTS
 QUADRANT = 32
 LIST_ROWS = 16
 HALF = S // 2
-QUARTER = HALF // 2
 RUN = 4
+PAIR = 2
 BANKS = 8
-PRE_SLOTS = 4
 
 
 def tile_list_hebbian_trace_update_kernel(
@@ -44,15 +43,10 @@ def tile_list_hebbian_trace_update_kernel(
             return sbuf.tile(shape, dtype, name=name, tag=tags[name], align_bytes=64)
 
         banks = []
-        pre_tiles = []
 
         def next_bank():
             banks.append(psum.tile([P, HALF], F32, name="acc", tag="bank%d" % (len(banks) % BANKS)))
             return banks[-1]
-
-        def next_pre():
-            pre_tiles.append(sbuf.tile([P, S], F32, name="pre", tag="pre%d" % (len(pre_tiles) % PRE_SLOTS)))
-            return pre_tiles[-1]
 
         list1 = sbuf.tile([P, S // LIST_ROWS], U16, name="list1")
         list2 = sbuf.tile([P, S // LIST_ROWS], U16, name="list2")
@@ -65,13 +59,12 @@ def tile_list_hebbian_trace_update_kernel(
         wb_w = held([P, H // 2], I32, "wb_w")
         wb_s = held([P, H // 4], I32, "wb_s")
         rates = sbuf.tile([P, 2, SLOTS], F32, name="rates")
-        g_tab = [held([P, T], F32, "g_tab%d" % q) for q in range(N // P)]
 
-        nc.gpsimd.memset(tab2_s[:], 0)
+        nc.vector.memset(tab2_s[:], 0)
         nc.vector.memset(tab_s[:], 0)
         nc.vector.memset(wb_s_raw[:], 0)
 
-        wa_raw, w_raw = {}, {}
+        wa_raw, w_raw, g_tab = {}, {}, {}
 
         def load_wa(a, b):
             wa_raw[(a, b)] = held([P, SLOTS, PASS], F32, "wa_raw%d%d" % (a, b))
@@ -86,7 +79,8 @@ def tile_list_hebbian_trace_update_kernel(
         def load_words(dst, words):
             nc.sync.dma_start(out=dst[:], in_=words.rearrange("p t i -> p (t i)").bitcast(I32))
 
-        def load_g(q):
+        def load_g(q, after=None):
+            g_tab[q] = held([P, T], F32, "g_tab%d" % q, after)
             nc.sync.dma_start(out=g_tab[q][:], in_=gT[q * P : (q + 1) * P, :])
 
         def load_plane(dst, rows):
@@ -101,88 +95,87 @@ def tile_list_hebbian_trace_update_kernel(
                     out=tab_s[first : first + 8, :], in_=tab_scales[:, 4 * u : 4 * u + 4, :].bitcast(I32)
                 )
 
-        nc.sync.dma_start(out=wb_w_raw[:], in_=wb_words[0].bitcast(I32))
         nc.sync.dma_start(list2[:], offs2)
         load_plane(tab2_s, tab2_scales[0])
-        load_words(tab2_w, tab2_words[0])
-        load_plane(wb_s_raw, wb_scales[0])
+        nc.sync.dma_start(out=wb_w_raw[:], in_=wb_words[0].bitcast(I32))
         nc.sync.dma_start(list1[:], offs)
-        load_words(tab_w[0], tab_words[0])
         load_wa(0, 0)
-        load_wa(1, 0)
         load_tab_planes()
+        load_wa(1, 0)
+        load_plane(wb_s_raw, wb_scales[0])
+        load_words(tab2_w, tab2_words[0])
+        load_words(tab_w[0], tab_words[0])
         load_words(tab_w[1], tab_words[1])
-        load_wa(1, 1)
-        load_wa(0, 1)
         nc.sync.dma_start(out=rates[:], in_=eta.rearrange("(b p t) -> p b t", b=2, t=SLOTS))
+        load_wa(0, 1)
+        load_wa(1, 1)
+        load_w(0, after="wa_raw00")
+        load_w(1, after="wa_raw10")
         load_g(0)
-        load_w(0, after="tab2_w")
-        load_g(1)
-        load_w(1, after="tab_w0")
-        load_g(2)
-        load_g(3)
+        load_g(1, after="tab_w0")
+        load_g(2, after="tab_w1")
+        load_g(3, after="wa_raw01")
+
+        half_cols = HALF // LIST_ROWS
+
+        def half_of(offsets, jh):
+            return offsets[:, jh * half_cols : (jh + 1) * half_cols]
 
         def halves(tile):
             return [tile[:, 0:HALF], tile[:, HALF:S]]
 
-        def gather(window, offsets, dtype, name, after=None):
-            picked = held([P, offsets.shape[1] * LIST_ROWS], dtype, name, after)
+        def gather(window, offsets, dtype, name):
+            picked = held([P, offsets.shape[1] * LIST_ROWS], dtype, name)
             nc.vector.tensor_copy(picked[:], window.indirect(offsets))
             return picked
 
-        def quantize(grouped, name):
-            codes = held([P, PASS], U32, name + "_codes")
+        def gather_halves(window, offsets, name):
+            return [gather(window, half_of(offsets, jh), U32, "%s%d" % (name, jh))[:] for jh in range(2)]
+
+        def quantize(grouped, name, after=None):
+            codes = held([P, PASS], U32, name + "_codes", after)
             scales = held([P, PASS], U8, name + "_scales")
             nc.vector.quantize_mx(out=codes[:].bitcast(FP8X4), scales=scales[:], in_=grouped[:])
             return codes, scales
 
-        def quantize_wa(a, b):
+        def group_wa(a, b, copy):
             grouped = held([P, SLOTS * PASS], BF16, "wa_grouped%d%d" % (a, b))
-            nc.vector.tensor_copy(
+            copy(
                 out=grouped[:].rearrange("p (t m j) -> p m j t", t=SLOTS, j=SLOTS),
                 in_=wa_raw[(a, b)][:].rearrange("p j (m t) -> p m j t", t=SLOTS),
             )
-            return quantize(grouped, "wa%d%d" % (a, b))
-
-        def interleave(rows, name, after=None, pieces=1):
-            grouped = held([P, SLOTS * PASS], BF16, name, after)
-            dst = grouped[:].rearrange("p (c i t) -> p c t i", t=SLOTS, i=RUN)
-            src = rows.rearrange("p t (c i) -> p c t i", i=RUN)
-            step = PASS // RUN // pieces
-            for u in range(pieces):
-                nc.scalar.copy(out=dst[:, u * step : (u + 1) * step], in_=src[:, u * step : (u + 1) * step])
             return grouped
 
-        v2_s = halves(gather(tab2_s[:].bitcast(U8), list2[:], U8, "v2_s"))
-        v2_w = halves(gather(tab2_w[:].bitcast(U32), list2[:], U32, "v2_w"))
+        def group_w(b, after):
+            grouped = held([P, SLOTS * PASS], BF16, "w_grouped%d" % b, after)
+            nc.scalar.copy(
+                out=grouped[:].rearrange("p (c i t) -> p c t i", t=SLOTS, i=RUN),
+                in_=w_raw[b][:].rearrange("p t (c i) -> p c t i", i=RUN),
+            )
+            return grouped
+
         nc.vector.tensor_copy(
             out=wb_w[:].bitcast(U16).rearrange("p (t m) -> p t m", t=SLOTS),
             in_=wb_w_raw[:].bitcast(U16).rearrange("p (m t) -> p t m", t=SLOTS),
         )
+        v2_s = halves(gather(tab2_s[:].bitcast(U8), list2[:], U8, "v2_s"))
+        v_s = halves(gather(tab_s[:].bitcast(U8), list1[:], U8, "v_s"))
         nc.vector.tensor_copy(
             out=wb_s[:].bitcast(U8).rearrange("p (t m) -> p t m", t=SLOTS),
             in_=wb_s_raw[:].bitcast(U8).rearrange("p (m t) -> p t m", t=SLOTS),
         )
-
-        wa_q = {}
+        wa_grouped, wa_q = {}, {}
+        for a in range(2):
+            wa_grouped[(a, 0)] = group_wa(a, 0, nc.scalar.copy)
+        wa_q[(0, 0)] = quantize(wa_grouped[(0, 0)], "wa00")
+        v2_w = gather_halves(tab2_w[:].bitcast(U32), list2, "v2_w")
+        wa_q[(1, 0)] = quantize(wa_grouped[(1, 0)], "wa10", after="tab2_w")
         v_w = [halves(gather(tab_w[0][:].bitcast(U32), list1[:], U32, "v_w0"))]
-        wa_q[(0, 0)] = quantize_wa(0, 0)
-        wa_q[(1, 0)] = quantize_wa(1, 0)
-        v_s = halves(gather(tab_s[:].bitcast(U8), list1[:], U8, "v_s"))
-        half_cols = HALF // LIST_ROWS
-        v_w.append(
-            [
-                gather(
-                    tab_w[1][:].bitcast(U32), list1[:, jh * half_cols : (jh + 1) * half_cols], U32, "v_w1%d" % jh
-                )[:]
-                for jh in range(2)
-            ]
-        )
-        wa_q[(1, 1)] = quantize_wa(1, 1)
-        wa_q[(0, 1)] = quantize_wa(0, 1)
+        v_w.append(gather_halves(tab_w[1][:].bitcast(U32), list1, "v_w1"))
 
-        post = {}
+        post = []
         for b in range(2):
+            post.append(held([P, 2, SLOTS, HALF], F32, "post%d" % b))
             for jh in range(2):
                 for t in range(SLOTS):
                     acc = next_bank()
@@ -196,94 +189,89 @@ def tile_list_hebbian_trace_update_kernel(
                         start=True,
                         stop=True,
                     )
-                    if jh == 0:
-                        post[(b, t)] = held([P, S], F32, "post%d%d" % (b, t))
-                    nc.scalar.activation(out=halves(post[(b, t)])[jh], in_=acc[:], func=TANH)
+                    nc.scalar.activation(out=post[b][:, jh, t, :], in_=acc[:], func=TANH)
 
-        def make_h(b, after):
-            flat = held([P, SLOTS, S], BF16, "flat%d" % b, after)
+        def scale_post(b):
             for t in range(SLOTS):
-                pre = next_pre()
-                for jh in range(2):
-                    acc = next_bank()
-                    for a in range(2):
-                        codes, scales = wa_q[(a, b)]
-                        nc.tensor.matmul_mx(
-                            out=acc[:],
-                            lhsT=codes[:, t * P : (t + 1) * P].bitcast(FP8X4),
-                            lhsT_scale=scales[:, t * P : (t + 1) * P],
-                            rhs=v_w[a][jh].bitcast(FP8X4),
-                            rhs_scale=v_s[jh][4 * (a + 1) : P, :],
-                            start=(a == 0),
-                            stop=(a == 1),
-                        )
-                    nc.scalar.activation(out=halves(pre)[jh], in_=acc[:], func=TANH)
-                nc.vector.scalar_tensor_tensor(
-                    out=flat[:, t, :],
-                    in0=pre[:],
-                    scalar=rates[:, b, t : t + 1],
-                    in1=post[(b, t)][:],
-                    op0=MULT,
-                    op1=MULT,
+                rows = post[b][:, :, t, :]
+                nc.vector.tensor_scalar(
+                    out=rows, in0=rows, scalar1=rates[:, b, t : t + 1], scalar2=None, op0=MULT
                 )
-            return [flat[:, :, 0:HALF], flat[:, :, HALF:S]]
 
-        def gather_g(q, after=None):
-            return halves(gather(g_tab[q][:], list1[:], F32, "g%d" % q, after))
+        scale_post(0)
+        for a in range(2):
+            wa_grouped[(a, 1)] = group_wa(a, 1, nc.vector.tensor_copy)
+        for a in range(2):
+            wa_q[(a, 1)] = quantize(wa_grouped[(a, 1)], "wa%d1" % a)
+        scale_post(1)
 
-        g = {}
-        h_flat = [make_h(0, after="wa_raw00")]
-        g[0] = gather_g(0)
-        h_flat.append(make_h(1, after="g_tab0"))
-
-        h_grouped, w_grouped = {}, {}
-        h_grouped[(0, 0)] = interleave(h_flat[0][0], "h_grouped00", after="wa_grouped00")
-        w_grouped[0] = interleave(w_raw[0][:], "w_grouped0", after="wa01_codes")
-        w_grouped[1] = interleave(w_raw[1][:], "w_grouped1")
-        h_grouped[(1, 0)] = interleave(h_flat[1][0], "h_grouped10", after="wa_grouped11")
-        h_grouped[(0, 1)] = interleave(h_flat[0][1], "h_grouped01", after="w_raw1")
-        h_grouped[(1, 1)] = interleave(h_flat[1][1], "h_grouped11", after="wa_grouped01", pieces=2)
-
-        h_q, w_q = {}, {}
-        g[1] = gather_g(1)
-        h_q[(0, 0)] = quantize(h_grouped[(0, 0)], "h00")
-        w_q[0] = quantize(w_grouped[0], "w0")
-        g[2] = gather_g(2)
-        w_q[1] = quantize(w_grouped[1], "w1")
-        h_q[(1, 0)] = quantize(h_grouped[(1, 0)], "h10")
-        g[3] = gather_g(3, after="h_grouped10")
-        h_q[(0, 1)] = quantize(h_grouped[(0, 1)], "h01")
-        last_codes = held([P, PASS], U32, "h11_codes")
-        last_scales = held([P, PASS], U8, "h11_scales")
-        for lo in (0, QUARTER):
-            nc.vector.quantize_mx(
-                out=last_codes[:, lo : lo + QUARTER].bitcast(FP8X4),
-                scales=last_scales[:, lo : lo + QUARTER],
-                in_=h_grouped[(1, 1)][:, SLOTS * lo : SLOTS * (lo + QUARTER)],
-            )
-        h_q[(1, 1)] = (last_codes, last_scales)
-
-        def finish(jh, lo, width, spent):
-            cols = slice(lo, lo + width)
-            for q in range(N // P):
+        def make_pre(b, jh, after=None):
+            pre = held([P, SLOTS, HALF], F32, "pre%d%d" % (b, jh), after)
+            for t in range(SLOTS):
                 acc = next_bank()
-                for b in range(2):
-                    w_codes, w_scales = w_q[b]
-                    h_codes, h_scales = h_q[(b, jh)]
+                for a in range(2):
+                    codes, scales = wa_q[(a, b)]
                     nc.tensor.matmul_mx(
-                        out=acc[:, 0:width],
-                        lhsT=w_codes[:, q * P : (q + 1) * P].bitcast(FP8X4),
-                        lhsT_scale=w_scales[:, q * P : (q + 1) * P],
-                        rhs=h_codes[:, cols].bitcast(FP8X4),
-                        rhs_scale=h_scales[:, cols],
-                        start=(b == 0),
-                        stop=(b == 1),
+                        out=acc[:],
+                        lhsT=codes[:, t * P : (t + 1) * P].bitcast(FP8X4),
+                        lhsT_scale=scales[:, t * P : (t + 1) * P],
+                        rhs=v_w[a][jh].bitcast(FP8X4),
+                        rhs_scale=v_s[jh][4 * (a + 1) : P, :],
+                        start=(a == 0),
+                        stop=(a == 1),
                     )
-                first = jh * HALF + lo
-                res = held([P, width], F32, "res%d_%d" % (q, first), spent[q])
-                nc.vector.tensor_tensor(out=res[:], in0=acc[:, 0:width], in1=g[q][jh][:, cols], op=ADD)
-                nc.sync.dma_start(out=out[q * P : (q + 1) * P, first : first + width], in_=res[:])
+                nc.scalar.activation(out=pre[:, t, :], in_=acc[:], func=TANH)
+            return pre
 
-        finish(0, 0, HALF, spent=["wa00_codes", "wa10_codes", "wb_w", "wa11_codes"])
-        finish(1, 0, QUARTER, spent=[None] * (N // P))
-        finish(1, QUARTER, QUARTER, spent=[None] * (N // P))
+        def make_h(pre, b, jh, after):
+            grouped = held([P, SLOTS * HALF], BF16, "h_grouped%d%d" % (b, jh), after)
+            nc.vector.tensor_tensor(
+                out=grouped[:].rearrange("p (c i t) -> p c t i", t=SLOTS, i=PAIR),
+                in0=pre[:].rearrange("p t (c i) -> p c t i", i=PAIR),
+                in1=post[b][:, jh, :, :].rearrange("p t (c i) -> p c t i", i=PAIR),
+                op=MULT,
+            )
+            return grouped
+
+        h_grouped, h_q, w_q = {}, {}, {}
+        for jh in range(2):
+            h_grouped[(0, jh)] = make_h(make_pre(0, jh), 0, jh, after="wa_grouped%d1" % jh)
+        for jh in range(2):
+            h_q[(0, jh)] = quantize(h_grouped[(0, jh)], "h0%d" % jh)
+        h_grouped[(1, 0)] = make_h(make_pre(1, 0, after="wa_raw11"), 1, 0, after="h_grouped00")
+        w_q[0] = quantize(group_w(0, after="wa_grouped00"), "w0")
+        h_q[(1, 0)] = quantize(h_grouped[(1, 0)], "h10")
+        w_q[1] = quantize(group_w(1, after="wa_grouped10"), "w1")
+        h_grouped[(1, 1)] = make_h(make_pre(1, 1, after="pre00"), 1, 1, after="h_grouped01")
+
+        def third_product(jh, q):
+            acc = next_bank()
+            for b in range(2):
+                w_codes, w_scales = w_q[b]
+                h_codes, h_scales = h_q[(b, jh)]
+                nc.tensor.matmul_mx(
+                    out=acc[:],
+                    lhsT=w_codes[:, q * P : (q + 1) * P].bitcast(FP8X4),
+                    lhsT_scale=w_scales[:, q * P : (q + 1) * P],
+                    rhs=h_codes[:].bitcast(FP8X4),
+                    rhs_scale=h_scales[:],
+                    start=(b == 0),
+                    stop=(b == 1),
+                )
+            sums = held([P, HALF], F32, "sums%d%d" % (jh, q))
+            nc.scalar.copy(out=sums[:], in_=acc[:])
+            return sums
+
+        def finish(jh, q, sums):
+            res = held([P, HALF], F32, "res%d%d" % (jh, q))
+            nc.vector.tensor_tensor(res[:], g_tab[q][:].indirect(half_of(list1, jh)), sums[:], ADD)
+            nc.sync.dma_start(out=out[q * P : (q + 1) * P, jh * HALF : (jh + 1) * HALF], in_=res[:])
+
+        first = [third_product(0, q) for q in range(N // P)]
+        finish(0, 0, first[0])
+        h_q[(1, 1)] = quantize(h_grouped[(1, 1)], "h11")
+        second = [third_product(1, q) for q in range(N // P)]
+        for q in range(1, N // P):
+            finish(0, q, first[q])
+        for q in range(N // P):
+            finish(1, q, second[q])

@@ -58,7 +58,7 @@ def tile_list_hebbian_trace_update_kernel(
         wb_s_raw = held([P, H // 4], I32, "wb_s_raw")
         wb_w = held([P, H // 2], I32, "wb_w")
         wb_s = held([P, H // 4], I32, "wb_s")
-        rates = sbuf.tile([P, 2, SLOTS], F32, name="rates")
+        rates = [[held([P, 1], F32, "rates%d%d" % (b, t)) for t in range(SLOTS)] for b in range(2)]
 
         nc.vector.memset(tab2_s[:], 0)
         nc.vector.memset(tab_s[:], 0)
@@ -73,8 +73,14 @@ def tile_list_hebbian_trace_update_kernel(
 
         def load_w(b, after):
             w_raw[b] = held([P, SLOTS, N], F32, "w_raw%d" % b, after)
-            rows = w[b * PASS : (b + 1) * PASS, :]
-            nc.sync.dma_start(out=w_raw[b][:], in_=rows.rearrange("(p t) n -> p t n", t=SLOTS))
+            rows = w[b * PASS : (b + 1) * PASS, :].rearrange("(m t i) n -> t m i n", t=SLOTS, i=RUN)
+            for t in range(SLOTS):
+                nc.sync.dma_start(out=w_raw[b][:, t, :], in_=rows[t])
+
+        def load_rates(b):
+            values = eta[b * PASS : (b + 1) * PASS].rearrange("(m t i) -> t m i", t=SLOTS, i=RUN)
+            for t in range(SLOTS):
+                nc.sync.dma_start(out=rates[b][t][:], in_=values[t])
 
         def load_words(dst, words):
             nc.sync.dma_start(out=dst[:], in_=words.rearrange("p t i -> p (t i)").bitcast(I32))
@@ -84,9 +90,9 @@ def tile_list_hebbian_trace_update_kernel(
             nc.sync.dma_start(out=g_tab[q][:], in_=gT[q * P : (q + 1) * P, :])
 
         def load_plane(dst, rows):
-            for u in range(P // QUADRANT):
-                first = QUADRANT * u
-                nc.sync.dma_start(out=dst[first : first + 4, :], in_=rows[4 * u : 4 * u + 4, :].bitcast(I32))
+            by_place = rows.rearrange("(u r) c -> r u c", r=4)
+            for r in range(4):
+                nc.sync.dma_start(out=dst[r:P:QUADRANT, :], in_=by_place[r].bitcast(I32))
 
         def load_tab_planes():
             for u in range(P // QUADRANT):
@@ -95,26 +101,27 @@ def tile_list_hebbian_trace_update_kernel(
                     out=tab_s[first : first + 8, :], in_=tab_scales[:, 4 * u : 4 * u + 4, :].bitcast(I32)
                 )
 
+        nc.sync.dma_start(out=wb_w_raw[:], in_=wb_words[0].bitcast(I32))
         nc.sync.dma_start(list2[:], offs2)
         load_plane(tab2_s, tab2_scales[0])
-        nc.sync.dma_start(out=wb_w_raw[:], in_=wb_words[0].bitcast(I32))
-        nc.sync.dma_start(list1[:], offs)
-        load_wa(0, 0)
-        load_tab_planes()
-        load_wa(1, 0)
-        load_plane(wb_s_raw, wb_scales[0])
         load_words(tab2_w, tab2_words[0])
+        nc.sync.dma_start(list1[:], offs)
+        load_plane(wb_s_raw, wb_scales[0])
         load_words(tab_w[0], tab_words[0])
         load_words(tab_w[1], tab_words[1])
-        nc.sync.dma_start(out=rates[:], in_=eta.rearrange("(b p t) -> p b t", b=2, t=SLOTS))
+        load_tab_planes()
+        load_rates(0)
+        load_rates(1)
+        load_wa(0, 0)
+        load_wa(1, 0)
         load_wa(0, 1)
         load_wa(1, 1)
-        load_w(0, after="wa_raw00")
-        load_w(1, after="wa_raw10")
-        load_g(0)
-        load_g(1, after="tab_w0")
-        load_g(2, after="tab_w1")
-        load_g(3, after="wa_raw01")
+        load_w(0, after="tab2_w")
+        load_w(1, after="tab_w0")
+        load_g(0, after="tab_w1")
+        load_g(1, after="wa_raw00")
+        load_g(2)
+        load_g(3)
 
         half_cols = HALF // LIST_ROWS
 
@@ -124,13 +131,10 @@ def tile_list_hebbian_trace_update_kernel(
         def halves(tile):
             return [tile[:, 0:HALF], tile[:, HALF:S]]
 
-        def gather(window, offsets, dtype, name):
-            picked = held([P, offsets.shape[1] * LIST_ROWS], dtype, name)
+        def gather(window, offsets, dtype, name, after=None):
+            picked = held([P, offsets.shape[1] * LIST_ROWS], dtype, name, after)
             nc.vector.tensor_copy(picked[:], window.indirect(offsets))
             return picked
-
-        def gather_halves(window, offsets, name):
-            return [gather(window, half_of(offsets, jh), U32, "%s%d" % (name, jh))[:] for jh in range(2)]
 
         def quantize(grouped, name, after=None):
             codes = held([P, PASS], U32, name + "_codes", after)
@@ -141,8 +145,8 @@ def tile_list_hebbian_trace_update_kernel(
         def group_wa(a, b, copy):
             grouped = held([P, SLOTS * PASS], BF16, "wa_grouped%d%d" % (a, b))
             copy(
-                out=grouped[:].rearrange("p (t m j) -> p m j t", t=SLOTS, j=SLOTS),
-                in_=wa_raw[(a, b)][:].rearrange("p j (m t) -> p m j t", t=SLOTS),
+                out=grouped[:].rearrange("p (t m i j) -> p t m j i", t=SLOTS, i=RUN, j=SLOTS),
+                in_=wa_raw[(a, b)][:].rearrange("p j (m t i) -> p t m j i", t=SLOTS, i=RUN),
             )
             return grouped
 
@@ -155,55 +159,63 @@ def tile_list_hebbian_trace_update_kernel(
             return grouped
 
         nc.vector.tensor_copy(
-            out=wb_w[:].bitcast(U16).rearrange("p (t m) -> p t m", t=SLOTS),
-            in_=wb_w_raw[:].bitcast(U16).rearrange("p (m t) -> p t m", t=SLOTS),
+            out=wb_w[:].rearrange("p (t m e) -> p t m e", t=SLOTS, e=2),
+            in_=wb_w_raw[:].rearrange("p (m t e) -> p t m e", t=SLOTS, e=2),
         )
         v2_s = halves(gather(tab2_s[:].bitcast(U8), list2[:], U8, "v2_s"))
-        v_s = halves(gather(tab_s[:].bitcast(U8), list1[:], U8, "v_s"))
         nc.vector.tensor_copy(
-            out=wb_s[:].bitcast(U8).rearrange("p (t m) -> p t m", t=SLOTS),
-            in_=wb_s_raw[:].bitcast(U8).rearrange("p (m t) -> p t m", t=SLOTS),
+            out=wb_s[:].rearrange("p (t m) -> p t m", t=SLOTS),
+            in_=wb_s_raw[:].rearrange("p (m t) -> p t m", t=SLOTS),
         )
-        wa_grouped, wa_q = {}, {}
+        v2_w = [
+            gather(tab2_w[:].bitcast(U32), half_of(list2, jh), U32, "v2_w%d" % jh, after)[:]
+            for jh, after in enumerate([None, "wb_s_raw"])
+        ]
+        v_w = [halves(gather(tab_w[a][:].bitcast(U32), list1[:], U32, "v_w%d" % a)) for a in range(2)]
+        v_s = halves(gather(tab_s[:].bitcast(U8), list1[:], U8, "v_s"))
+
+        def make_post(b, jh, dst):
+            for t in range(SLOTS):
+                acc = next_bank()
+                col = (2 * t + b) * P
+                nc.tensor.matmul_mx(
+                    out=acc[:],
+                    lhsT=wb_w[:].bitcast(U8)[:, 2 * col : 2 * (col + P)].bitcast(FP4X4),
+                    lhsT_scale=wb_s[:].bitcast(U8)[:, col : col + P],
+                    rhs=v2_w[jh].bitcast(FP8X4),
+                    rhs_scale=v2_s[jh],
+                    start=True,
+                    stop=True,
+                )
+                nc.scalar.activation(out=dst[:, t, :], in_=acc[:], func=TANH)
+
+        def scale_post(rows, b, t):
+            nc.vector.tensor_scalar(out=rows, in0=rows, scalar1=rates[b][t][:], scalar2=None, op0=MULT)
+
+        post, wa_grouped, wa_q = {}, {}, {}
+        both = held([P, 2, SLOTS, HALF], F32, "post0")
+        for jh in range(2):
+            post[(0, jh)] = both[:, jh, :, :]
+            make_post(0, jh, post[(0, jh)])
+        post[(1, 0)] = held([P, SLOTS, HALF], F32, "post10")[:]
+        make_post(1, 0, post[(1, 0)])
         for a in range(2):
             wa_grouped[(a, 0)] = group_wa(a, 0, nc.scalar.copy)
-        wa_q[(0, 0)] = quantize(wa_grouped[(0, 0)], "wa00")
-        v2_w = gather_halves(tab2_w[:].bitcast(U32), list2, "v2_w")
-        wa_q[(1, 0)] = quantize(wa_grouped[(1, 0)], "wa10", after="tab2_w")
-        v_w = [halves(gather(tab_w[0][:].bitcast(U32), list1[:], U32, "v_w0"))]
-        v_w.append(gather_halves(tab_w[1][:].bitcast(U32), list1, "v_w1"))
+        post[(1, 1)] = held([P, SLOTS, HALF], F32, "post11", after="wa_raw10")[:]
+        make_post(1, 1, post[(1, 1)])
 
-        post = []
-        for b in range(2):
-            post.append(held([P, 2, SLOTS, HALF], F32, "post%d" % b))
-            for jh in range(2):
-                for t in range(SLOTS):
-                    acc = next_bank()
-                    col = (2 * t + b) * P
-                    nc.tensor.matmul_mx(
-                        out=acc[:],
-                        lhsT=wb_w[:].bitcast(U8)[:, 2 * col : 2 * (col + P)].bitcast(FP4X4),
-                        lhsT_scale=wb_s[:].bitcast(U8)[:, col : col + P],
-                        rhs=v2_w[jh].bitcast(FP8X4),
-                        rhs_scale=v2_s[jh],
-                        start=True,
-                        stop=True,
-                    )
-                    nc.scalar.activation(out=post[b][:, jh, t, :], in_=acc[:], func=TANH)
-
-        def scale_post(b):
-            for t in range(SLOTS):
-                rows = post[b][:, :, t, :]
-                nc.vector.tensor_scalar(
-                    out=rows, in0=rows, scalar1=rates[:, b, t : t + 1], scalar2=None, op0=MULT
-                )
-
-        scale_post(0)
+        for t in range(SLOTS):
+            scale_post(both[:, :, t, :], 0, t)
+        for t in range(SLOTS):
+            scale_post(post[(1, 0)][:, t, :], 1, t)
         for a in range(2):
-            wa_grouped[(a, 1)] = group_wa(a, 1, nc.vector.tensor_copy)
-        for a in range(2):
-            wa_q[(a, 1)] = quantize(wa_grouped[(a, 1)], "wa%d1" % a)
-        scale_post(1)
+            wa_q[(a, 0)] = quantize(wa_grouped[(a, 0)], "wa%d0" % a)
+        wa_grouped[(0, 1)] = group_wa(0, 1, nc.vector.tensor_copy)
+        for t in range(SLOTS):
+            scale_post(post[(1, 1)][:, t, :], 1, t)
+        wa_q[(0, 1)] = quantize(wa_grouped[(0, 1)], "wa01")
+        wa_grouped[(1, 1)] = group_wa(1, 1, nc.vector.tensor_copy)
+        wa_q[(1, 1)] = quantize(wa_grouped[(1, 1)], "wa11")
 
         def make_pre(b, jh, after=None):
             pre = held([P, SLOTS, HALF], F32, "pre%d%d" % (b, jh), after)
@@ -228,21 +240,22 @@ def tile_list_hebbian_trace_update_kernel(
             nc.vector.tensor_tensor(
                 out=grouped[:].rearrange("p (c i t) -> p c t i", t=SLOTS, i=PAIR),
                 in0=pre[:].rearrange("p t (c i) -> p c t i", i=PAIR),
-                in1=post[b][:, jh, :, :].rearrange("p t (c i) -> p c t i", i=PAIR),
+                in1=post[(b, jh)].rearrange("p t (c i) -> p c t i", i=PAIR),
                 op=MULT,
             )
             return grouped
 
         h_grouped, h_q, w_q = {}, {}, {}
-        for jh in range(2):
-            h_grouped[(0, jh)] = make_h(make_pre(0, jh), 0, jh, after="wa_grouped%d1" % jh)
+        for jh, after in enumerate(["wa_raw11", "wa_grouped11"]):
+            h_grouped[(0, jh)] = make_h(make_pre(0, jh), 0, jh, after)
         for jh in range(2):
             h_q[(0, jh)] = quantize(h_grouped[(0, jh)], "h0%d" % jh)
-        h_grouped[(1, 0)] = make_h(make_pre(1, 0, after="wa_raw11"), 1, 0, after="h_grouped00")
-        w_q[0] = quantize(group_w(0, after="wa_grouped00"), "w0")
+        h_grouped[(1, 0)] = make_h(make_pre(1, 0, after="wa_raw01"), 1, 0, after="h_grouped00")
+        w_q[0] = quantize(group_w(0, after="wa01_codes"), "w0")
         h_q[(1, 0)] = quantize(h_grouped[(1, 0)], "h10")
-        w_q[1] = quantize(group_w(1, after="wa_grouped10"), "w1")
         h_grouped[(1, 1)] = make_h(make_pre(1, 1, after="pre00"), 1, 1, after="h_grouped01")
+        w_q[1] = quantize(group_w(1, after="wa_grouped10"), "w1")
+        h_q[(1, 1)] = quantize(h_grouped[(1, 1)], "h11")
 
         def third_product(jh, q):
             acc = next_bank()
@@ -267,11 +280,6 @@ def tile_list_hebbian_trace_update_kernel(
             nc.vector.tensor_tensor(res[:], g_tab[q][:].indirect(half_of(list1, jh)), sums[:], ADD)
             nc.sync.dma_start(out=out[q * P : (q + 1) * P, jh * HALF : (jh + 1) * HALF], in_=res[:])
 
-        first = [third_product(0, q) for q in range(N // P)]
-        finish(0, 0, first[0])
-        h_q[(1, 1)] = quantize(h_grouped[(1, 1)], "h11")
-        second = [third_product(1, q) for q in range(N // P)]
-        for q in range(1, N // P):
-            finish(0, q, first[q])
         for q in range(N // P):
-            finish(1, q, second[q])
+            for jh in range(2):
+                finish(jh, q, third_product(jh, q))

@@ -108,11 +108,11 @@ def tile_list_hebbian_trace_update_kernel(
         nc.sync.dma_start(list1[:], offs)
         load_plane(wb_s_raw, wb_scales[0])
         load_words(tab_w[0], tab_words[0])
-        load_words(tab_w[1], tab_words[1])
         load_tab_planes()
+        load_words(tab_w[1], tab_words[1])
         load_rates(0)
-        load_rates(1)
         load_wa(0, 0)
+        load_rates(1)
         load_wa(1, 0)
         load_wa(0, 1)
         load_wa(1, 1)
@@ -150,12 +150,13 @@ def tile_list_hebbian_trace_update_kernel(
             )
             return grouped
 
-        def group_w(b, after):
+        def group_w(b, after, copies):
             grouped = held([P, SLOTS * PASS], BF16, "w_grouped%d" % b, after)
-            nc.scalar.copy(
-                out=grouped[:].rearrange("p (c i t) -> p c t i", t=SLOTS, i=RUN),
-                in_=w_raw[b][:].rearrange("p t (c i) -> p c t i", i=RUN),
-            )
+            dst = grouped[:].rearrange("p (c i t) -> p c t i", t=SLOTS, i=RUN)
+            src = w_raw[b][:].rearrange("p t (c i) -> p c t i", i=RUN)
+            share = N // RUN // len(copies)
+            for u, copy in enumerate(copies):
+                copy(out=dst[:, u * share : (u + 1) * share], in_=src[:, u * share : (u + 1) * share])
             return grouped
 
         nc.vector.tensor_copy(
@@ -171,8 +172,9 @@ def tile_list_hebbian_trace_update_kernel(
             gather(tab2_w[:].bitcast(U32), half_of(list2, jh), U32, "v2_w%d" % jh, after)[:]
             for jh, after in enumerate([None, "wb_s_raw"])
         ]
-        v_w = [halves(gather(tab_w[a][:].bitcast(U32), list1[:], U32, "v_w%d" % a)) for a in range(2)]
+        v_w = [halves(gather(tab_w[0][:].bitcast(U32), list1[:], U32, "v_w0"))]
         v_s = halves(gather(tab_s[:].bitcast(U8), list1[:], U8, "v_s"))
+        v_w.append(halves(gather(tab_w[1][:].bitcast(U32), list1[:], U32, "v_w1")))
 
         def make_post(b, jh, dst):
             for t in range(SLOTS):
@@ -193,9 +195,9 @@ def tile_list_hebbian_trace_update_kernel(
             nc.vector.tensor_scalar(out=rows, in0=rows, scalar1=rates[b][t][:], scalar2=None, op0=MULT)
 
         post, wa_grouped, wa_q = {}, {}, {}
-        both = held([P, 2, SLOTS, HALF], F32, "post0")
+        both = held([P, SLOTS, S], F32, "post0")
         for jh in range(2):
-            post[(0, jh)] = both[:, jh, :, :]
+            post[(0, jh)] = both[:, :, jh * HALF : (jh + 1) * HALF]
             make_post(0, jh, post[(0, jh)])
         post[(1, 0)] = held([P, SLOTS, HALF], F32, "post10")[:]
         make_post(1, 0, post[(1, 0)])
@@ -205,7 +207,7 @@ def tile_list_hebbian_trace_update_kernel(
         make_post(1, 1, post[(1, 1)])
 
         for t in range(SLOTS):
-            scale_post(both[:, :, t, :], 0, t)
+            scale_post(both[:, t, :], 0, t)
         for t in range(SLOTS):
             scale_post(post[(1, 0)][:, t, :], 1, t)
         for a in range(2):
@@ -251,35 +253,42 @@ def tile_list_hebbian_trace_update_kernel(
         for jh in range(2):
             h_q[(0, jh)] = quantize(h_grouped[(0, jh)], "h0%d" % jh)
         h_grouped[(1, 0)] = make_h(make_pre(1, 0, after="wa_raw01"), 1, 0, after="h_grouped00")
-        w_q[0] = quantize(group_w(0, after="wa01_codes"), "w0")
+        w_q[0] = quantize(group_w(0, "wa01_codes", [nc.scalar.copy]), "w0")
         h_q[(1, 0)] = quantize(h_grouped[(1, 0)], "h10")
-        h_grouped[(1, 1)] = make_h(make_pre(1, 1, after="pre00"), 1, 1, after="h_grouped01")
-        w_q[1] = quantize(group_w(1, after="wa_grouped10"), "w1")
+        last_pre = make_pre(1, 1, after="pre00")
+        w_grouped = group_w(1, "wa_grouped10", [nc.scalar.copy])
+        h_grouped[(1, 1)] = make_h(last_pre, 1, 1, after="h_grouped01")
+        w_q[1] = quantize(w_grouped, "w1")
         h_q[(1, 1)] = quantize(h_grouped[(1, 1)], "h11")
 
-        def third_product(jh, q):
-            acc = next_bank()
-            for b in range(2):
-                w_codes, w_scales = w_q[b]
-                h_codes, h_scales = h_q[(b, jh)]
-                nc.tensor.matmul_mx(
-                    out=acc[:],
-                    lhsT=w_codes[:, q * P : (q + 1) * P].bitcast(FP8X4),
-                    lhsT_scale=w_scales[:, q * P : (q + 1) * P],
-                    rhs=h_codes[:].bitcast(FP8X4),
-                    rhs_scale=h_scales[:],
-                    start=(b == 0),
-                    stop=(b == 1),
-                )
-            sums = held([P, HALF], F32, "sums%d%d" % (jh, q))
-            nc.scalar.copy(out=sums[:], in_=acc[:])
+        def third_product(q):
+            sums = held([P, S], F32, "sums%d" % q)
+            for jh in range(2):
+                acc = next_bank()
+                for b in range(2):
+                    w_codes, w_scales = w_q[b]
+                    h_codes, h_scales = h_q[(b, jh)]
+                    nc.tensor.matmul_mx(
+                        out=acc[:],
+                        lhsT=w_codes[:, q * P : (q + 1) * P].bitcast(FP8X4),
+                        lhsT_scale=w_scales[:, q * P : (q + 1) * P],
+                        rhs=h_codes[:].bitcast(FP8X4),
+                        rhs_scale=h_scales[:],
+                        start=(b == 0),
+                        stop=(b == 1),
+                    )
+                nc.scalar.copy(out=halves(sums)[jh], in_=acc[:])
             return sums
 
-        def finish(jh, q, sums):
-            res = held([P, HALF], F32, "res%d%d" % (jh, q))
-            nc.vector.tensor_tensor(res[:], g_tab[q][:].indirect(half_of(list1, jh)), sums[:], ADD)
-            nc.sync.dma_start(out=out[q * P : (q + 1) * P, jh * HALF : (jh + 1) * HALF], in_=res[:])
+        def finish(q, sums, widths):
+            first = 0
+            for width in widths:
+                res = held([P, width], F32, "res%d_%d" % (q, first))
+                offsets = list1[:, first // LIST_ROWS : (first + width) // LIST_ROWS]
+                nc.vector.tensor_tensor(res[:], g_tab[q][:].indirect(offsets), sums[:, first : first + width], ADD)
+                nc.sync.dma_start(out=out[q * P : (q + 1) * P, first : first + width], in_=res[:])
+                first = first + width
 
+        widths = [[HALF, HALF], [S], [S], [HALF, HALF // 2, HALF // 2]]
         for q in range(N // P):
-            for jh in range(2):
-                finish(jh, q, third_product(jh, q))
+            finish(q, third_product(q), widths[q])

@@ -108,9 +108,9 @@ def tile_list_hebbian_trace_update_kernel(
         nc.sync.dma_start(list1[:], offs)
         load_plane(wb_s_raw, wb_scales[0])
         load_words(tab_w[0], tab_words[0])
-        load_tab_planes()
-        load_words(tab_w[1], tab_words[1])
         load_rates(0)
+        load_words(tab_w[1], tab_words[1])
+        load_tab_planes()
         load_wa(0, 0)
         load_rates(1)
         load_wa(1, 0)
@@ -119,7 +119,7 @@ def tile_list_hebbian_trace_update_kernel(
         load_w(0, after="tab2_w")
         load_w(1, after="tab_w0")
         load_g(0, after="tab_w1")
-        load_g(1, after="wa_raw00")
+        load_g(1)
         load_g(2)
         load_g(3)
 
@@ -172,9 +172,8 @@ def tile_list_hebbian_trace_update_kernel(
             gather(tab2_w[:].bitcast(U32), half_of(list2, jh), U32, "v2_w%d" % jh, after)[:]
             for jh, after in enumerate([None, "wb_s_raw"])
         ]
-        v_w = [halves(gather(tab_w[0][:].bitcast(U32), list1[:], U32, "v_w0"))]
+        v_w = [halves(gather(tab_w[a][:].bitcast(U32), list1[:], U32, "v_w%d" % a)) for a in range(2)]
         v_s = halves(gather(tab_s[:].bitcast(U8), list1[:], U8, "v_s"))
-        v_w.append(halves(gather(tab_w[1][:].bitcast(U32), list1[:], U32, "v_w1")))
 
         def make_post(b, jh, dst):
             for t in range(SLOTS):
@@ -191,30 +190,33 @@ def tile_list_hebbian_trace_update_kernel(
                 )
                 nc.scalar.activation(out=dst[:, t, :], in_=acc[:], func=TANH)
 
-        def scale_post(rows, b, t):
-            nc.vector.tensor_scalar(out=rows, in0=rows, scalar1=rates[b][t][:], scalar2=None, op0=MULT)
+        def scale_post(dst, src, b):
+            for t in range(SLOTS):
+                nc.vector.tensor_scalar(
+                    out=dst[:, t, :], in0=src[:, t, :], scalar1=rates[b][t][:], scalar2=None, op0=MULT
+                )
 
         post, wa_grouped, wa_q = {}, {}, {}
         both = held([P, SLOTS, S], F32, "post0")
         for jh in range(2):
             post[(0, jh)] = both[:, :, jh * HALF : (jh + 1) * HALF]
             make_post(0, jh, post[(0, jh)])
+            for t in range(SLOTS):
+                rows = post[(0, jh)][:, t, :]
+                nc.gpsimd.tensor_scalar(out=rows, in0=rows, scalar1=rates[0][t][:], scalar2=0.0, op0=MULT, op1=ADD)
         post[(1, 0)] = held([P, SLOTS, HALF], F32, "post10")[:]
         make_post(1, 0, post[(1, 0)])
-        for a in range(2):
-            wa_grouped[(a, 0)] = group_wa(a, 0, nc.scalar.copy)
-        post[(1, 1)] = held([P, SLOTS, HALF], F32, "post11", after="wa_raw10")[:]
-        make_post(1, 1, post[(1, 1)])
+        wa_grouped[(0, 0)] = group_wa(0, 0, nc.scalar.copy)
+        unscaled = held([P, SLOTS, HALF], F32, "unscaled11", after="wa_raw00")
+        make_post(1, 1, unscaled)
 
-        for t in range(SLOTS):
-            scale_post(both[:, t, :], 0, t)
-        for t in range(SLOTS):
-            scale_post(post[(1, 0)][:, t, :], 1, t)
-        for a in range(2):
-            wa_q[(a, 0)] = quantize(wa_grouped[(a, 0)], "wa%d0" % a)
+        scale_post(post[(1, 0)], post[(1, 0)], 1)
+        wa_grouped[(1, 0)] = group_wa(1, 0, nc.vector.tensor_copy)
+        wa_q[(0, 0)] = quantize(wa_grouped[(0, 0)], "wa00", after="wa_raw10")
+        wa_q[(1, 0)] = quantize(wa_grouped[(1, 0)], "wa10")
         wa_grouped[(0, 1)] = group_wa(0, 1, nc.vector.tensor_copy)
-        for t in range(SLOTS):
-            scale_post(post[(1, 1)][:, t, :], 1, t)
+        post[(1, 1)] = held([P, SLOTS, HALF], F32, "post11", after="wa_raw01")[:]
+        scale_post(post[(1, 1)], unscaled, 1)
         wa_q[(0, 1)] = quantize(wa_grouped[(0, 1)], "wa01")
         wa_grouped[(1, 1)] = group_wa(1, 1, nc.vector.tensor_copy)
         wa_q[(1, 1)] = quantize(wa_grouped[(1, 1)], "wa11")
@@ -252,43 +254,45 @@ def tile_list_hebbian_trace_update_kernel(
             h_grouped[(0, jh)] = make_h(make_pre(0, jh), 0, jh, after)
         for jh in range(2):
             h_q[(0, jh)] = quantize(h_grouped[(0, jh)], "h0%d" % jh)
-        h_grouped[(1, 0)] = make_h(make_pre(1, 0, after="wa_raw01"), 1, 0, after="h_grouped00")
-        w_q[0] = quantize(group_w(0, "wa01_codes", [nc.scalar.copy]), "w0")
+        w_grouped = [group_w(0, "wa_grouped00", [nc.scalar.copy])]
+        h_grouped[(1, 0)] = make_h(make_pre(1, 0, after="w_raw0"), 1, 0, after="h_grouped00")
+        w_q[0] = quantize(w_grouped[0], "w0")
+        w_grouped.append(group_w(1, "wa_grouped10", [nc.scalar.copy]))
         h_q[(1, 0)] = quantize(h_grouped[(1, 0)], "h10")
-        last_pre = make_pre(1, 1, after="pre00")
-        w_grouped = group_w(1, "wa_grouped10", [nc.scalar.copy])
-        h_grouped[(1, 1)] = make_h(last_pre, 1, 1, after="h_grouped01")
-        w_q[1] = quantize(w_grouped, "w1")
-        h_q[(1, 1)] = quantize(h_grouped[(1, 1)], "h11")
+        w_q[1] = quantize(w_grouped[1], "w1")
+        h_grouped[(1, 1)] = make_h(make_pre(1, 1, after="pre00"), 1, 1, after="h_grouped01")
 
-        def third_product(q):
-            sums = held([P, S], F32, "sums%d" % q)
-            for jh in range(2):
-                acc = next_bank()
-                for b in range(2):
-                    w_codes, w_scales = w_q[b]
-                    h_codes, h_scales = h_q[(b, jh)]
-                    nc.tensor.matmul_mx(
-                        out=acc[:],
-                        lhsT=w_codes[:, q * P : (q + 1) * P].bitcast(FP8X4),
-                        lhsT_scale=w_scales[:, q * P : (q + 1) * P],
-                        rhs=h_codes[:].bitcast(FP8X4),
-                        rhs_scale=h_scales[:],
-                        start=(b == 0),
-                        stop=(b == 1),
-                    )
-                nc.scalar.copy(out=halves(sums)[jh], in_=acc[:])
-            return sums
+        sums = [held([P, S], F32, "sums%d" % q) for q in range(N // P)]
 
-        def finish(q, sums, widths):
-            first = 0
-            for width in widths:
-                res = held([P, width], F32, "res%d_%d" % (q, first))
-                offsets = list1[:, first // LIST_ROWS : (first + width) // LIST_ROWS]
-                nc.vector.tensor_tensor(res[:], g_tab[q][:].indirect(offsets), sums[:, first : first + width], ADD)
-                nc.sync.dma_start(out=out[q * P : (q + 1) * P, first : first + width], in_=res[:])
-                first = first + width
+        def third_product(q, jh):
+            acc = next_bank()
+            for b in range(2):
+                w_codes, w_scales = w_q[b]
+                h_codes, h_scales = h_q[(b, jh)]
+                nc.tensor.matmul_mx(
+                    out=acc[:],
+                    lhsT=w_codes[:, q * P : (q + 1) * P].bitcast(FP8X4),
+                    lhsT_scale=w_scales[:, q * P : (q + 1) * P],
+                    rhs=h_codes[:].bitcast(FP8X4),
+                    rhs_scale=h_scales[:],
+                    start=(b == 0),
+                    stop=(b == 1),
+                )
+            nc.scalar.copy(out=halves(sums[q])[jh], in_=acc[:])
 
-        widths = [[HALF, HALF], [S], [S], [HALF, HALF // 2, HALF // 2]]
+        def finish(q, first, width):
+            res = held([P, width], F32, "res%d_%d" % (q, first))
+            offsets = list1[:, first // LIST_ROWS : (first + width) // LIST_ROWS]
+            nc.vector.tensor_tensor(res[:], g_tab[q][:].indirect(offsets), sums[q][:, first : first + width], ADD)
+            nc.sync.dma_start(out=out[q * P : (q + 1) * P, first : first + width], in_=res[:])
+
         for q in range(N // P):
-            finish(q, third_product(q), widths[q])
+            third_product(q, 0)
+            finish(q, 0, HALF)
+            if q == 0:
+                h_q[(1, 1)] = quantize(h_grouped[(1, 1)], "h11")
+        for q in range(N // P):
+            third_product(q, 1)
+            widths = [HALF] if q < N // P - 1 else [HALF // 2, HALF // 2]
+            for u, width in enumerate(widths):
+                finish(q, HALF + u * width, width)

@@ -204,16 +204,17 @@ def tile_list_hebbian_trace_update_kernel(
             for t in range(SLOTS):
                 rows = post[(0, jh)][:, t, :]
                 nc.gpsimd.tensor_scalar(out=rows, in0=rows, scalar1=rates[0][t][:], scalar2=0.0, op0=MULT, op1=ADD)
-        post[(1, 0)] = held([P, SLOTS, HALF], F32, "post10")[:]
-        make_post(1, 0, post[(1, 0)])
+        unscaled10 = held([P, SLOTS, HALF], F32, "unscaled10")
+        make_post(1, 0, unscaled10)
         wa_grouped[(0, 0)] = group_wa(0, 0, nc.scalar.copy)
         unscaled = held([P, SLOTS, HALF], F32, "unscaled11", after="wa_raw00")
         make_post(1, 1, unscaled)
 
-        scale_post(post[(1, 0)], post[(1, 0)], 1)
         wa_grouped[(1, 0)] = group_wa(1, 0, nc.vector.tensor_copy)
-        wa_q[(0, 0)] = quantize(wa_grouped[(0, 0)], "wa00", after="wa_raw10")
         wa_q[(1, 0)] = quantize(wa_grouped[(1, 0)], "wa10")
+        wa_q[(0, 0)] = quantize(wa_grouped[(0, 0)], "wa00", after="wa_raw10")
+        post[(1, 0)] = held([P, SLOTS, HALF], F32, "post10", after="wa_grouped00")[:]
+        scale_post(post[(1, 0)], unscaled10, 1)
         wa_grouped[(0, 1)] = group_wa(0, 1, nc.vector.tensor_copy)
         post[(1, 1)] = held([P, SLOTS, HALF], F32, "post11", after="wa_raw01")[:]
         scale_post(post[(1, 1)], unscaled, 1)
@@ -223,9 +224,10 @@ def tile_list_hebbian_trace_update_kernel(
 
         def make_pre(b, jh, after=None):
             pre = held([P, SLOTS, HALF], F32, "pre%d%d" % (b, jh), after)
+            order = (1 - b, b)
             for t in range(SLOTS):
                 acc = next_bank()
-                for a in range(2):
+                for a in order:
                     codes, scales = wa_q[(a, b)]
                     nc.tensor.matmul_mx(
                         out=acc[:],
@@ -233,8 +235,8 @@ def tile_list_hebbian_trace_update_kernel(
                         lhsT_scale=scales[:, t * P : (t + 1) * P],
                         rhs=v_w[a][jh].bitcast(FP8X4),
                         rhs_scale=v_s[jh][4 * (a + 1) : P, :],
-                        start=(a == 0),
-                        stop=(a == 1),
+                        start=(a == order[0]),
+                        stop=(a == order[1]),
                     )
                 nc.scalar.activation(out=pre[:, t, :], in_=acc[:], func=TANH)
             return pre
@@ -254,7 +256,7 @@ def tile_list_hebbian_trace_update_kernel(
             h_grouped[(0, jh)] = make_h(make_pre(0, jh), 0, jh, after)
         for jh in range(2):
             h_q[(0, jh)] = quantize(h_grouped[(0, jh)], "h0%d" % jh)
-        w_grouped = [group_w(0, "wa_grouped00", [nc.scalar.copy])]
+        w_grouped = [group_w(0, "wa_grouped01", [nc.scalar.copy])]
         h_grouped[(1, 0)] = make_h(make_pre(1, 0, after="w_raw0"), 1, 0, after="h_grouped00")
         w_q[0] = quantize(w_grouped[0], "w0")
         w_grouped.append(group_w(1, "wa_grouped10", [nc.scalar.copy]))

@@ -25,6 +25,7 @@ LIST_ROWS = 16
 HALF = S // 2
 RUN = 4
 PAIR = 2
+WARM_UPS = 4
 BANKS = 8
 
 
@@ -58,7 +59,8 @@ def tile_list_hebbian_trace_update_kernel(
         wb_s_raw = held([P, H // 4], I32, "wb_s_raw")
         wb_w = held([P, H // 2], I32, "wb_w")
         wb_s = held([P, H // 4], I32, "wb_s")
-        rates = [[held([P, 1], F32, "rates%d%d" % (b, t)) for t in range(SLOTS)] for b in range(2)]
+        rate_runs = held([P, 2, 16], F32, "rate_runs")
+        rates = [[rate_runs[:, b, RUN * t : RUN * t + 1] for t in range(SLOTS)] for b in range(2)]
 
         nc.vector.memset(tab2_s[:], 0)
         nc.vector.memset(tab_s[:], 0)
@@ -77,10 +79,10 @@ def tile_list_hebbian_trace_update_kernel(
             for t in range(SLOTS):
                 nc.sync.dma_start(out=w_raw[b][:, t, :], in_=rows[t])
 
-        def load_rates(b):
-            values = eta[b * PASS : (b + 1) * PASS].rearrange("(m t i) -> t m i", t=SLOTS, i=RUN)
-            for t in range(SLOTS):
-                nc.sync.dma_start(out=rates[b][t][:], in_=values[t])
+        def load_rates():
+            groups = eta.rearrange("(b m x) -> m b x", b=2, x=16)
+            for i in range(RUN):
+                nc.sync.dma_start(out=rate_runs[i:P:RUN, :, 0:13], in_=groups[:, :, i : i + 13])
 
         def load_words(dst, words):
             nc.sync.dma_start(out=dst[:], in_=words.rearrange("p t i -> p (t i)").bitcast(I32))
@@ -94,12 +96,11 @@ def tile_list_hebbian_trace_update_kernel(
             for r in range(4):
                 nc.sync.dma_start(out=dst[r:P:QUADRANT, :], in_=by_place[r].bitcast(I32))
 
-        def load_tab_planes():
-            for u in range(P // QUADRANT):
-                first = QUADRANT * u + 4
-                nc.sync.dma_start(
-                    out=tab_s[first : first + 8, :], in_=tab_scales[:, 4 * u : 4 * u + 4, :].bitcast(I32)
-                )
+        def load_tab_planes(places):
+            for r in places:
+                for a in range(2):
+                    by_place = tab_scales[a].rearrange("(u r) c -> r u c", r=4)
+                    nc.sync.dma_start(out=tab_s[4 * (a + 1) + r : P : QUADRANT, :], in_=by_place[r].bitcast(I32))
 
         nc.sync.dma_start(out=wb_w_raw[:], in_=wb_words[0].bitcast(I32))
         nc.sync.dma_start(list2[:], offs2)
@@ -108,11 +109,11 @@ def tile_list_hebbian_trace_update_kernel(
         nc.sync.dma_start(list1[:], offs)
         load_plane(wb_s_raw, wb_scales[0])
         load_words(tab_w[0], tab_words[0])
-        load_rates(0)
+        load_rates()
+        load_tab_planes([0])
         load_words(tab_w[1], tab_words[1])
-        load_tab_planes()
+        load_tab_planes([1, 2, 3])
         load_wa(0, 0)
-        load_rates(1)
         load_wa(1, 0)
         load_wa(0, 1)
         load_wa(1, 1)
@@ -142,12 +143,12 @@ def tile_list_hebbian_trace_update_kernel(
             nc.vector.quantize_mx(out=codes[:].bitcast(FP8X4), scales=scales[:], in_=grouped[:])
             return codes, scales
 
-        def group_wa(a, b, copy):
+        def group_wa(a, b, shares):
             grouped = held([P, SLOTS * PASS], BF16, "wa_grouped%d%d" % (a, b))
-            copy(
-                out=grouped[:].rearrange("p (t m i j) -> p t m j i", t=SLOTS, i=RUN, j=SLOTS),
-                in_=wa_raw[(a, b)][:].rearrange("p j (m t i) -> p t m j i", t=SLOTS, i=RUN),
-            )
+            dst = grouped[:].rearrange("p (t m i j) -> p t m j i", t=SLOTS, i=RUN, j=SLOTS)
+            src = wa_raw[(a, b)][:].rearrange("p j (m t i) -> p t m j i", t=SLOTS, i=RUN)
+            for copy, first, end in shares:
+                copy(out=dst[:, first:end], in_=src[:, first:end])
             return grouped
 
         def group_w(b, after, copies):
@@ -193,40 +194,52 @@ def tile_list_hebbian_trace_update_kernel(
         def scale_post(dst, src, b):
             for t in range(SLOTS):
                 nc.vector.tensor_scalar(
-                    out=dst[:, t, :], in0=src[:, t, :], scalar1=rates[b][t][:], scalar2=None, op0=MULT
+                    out=dst[:, t, :], in0=src[:, t, :], scalar1=rates[b][t], scalar2=None, op0=MULT
                 )
 
         post, wa_grouped, wa_q = {}, {}, {}
+        on_vector = [(nc.vector.tensor_copy, 0, SLOTS)]
         both = held([P, SLOTS, S], F32, "post0")
         for jh in range(2):
             post[(0, jh)] = both[:, :, jh * HALF : (jh + 1) * HALF]
             make_post(0, jh, post[(0, jh)])
             for t in range(SLOTS):
                 rows = post[(0, jh)][:, t, :]
-                nc.gpsimd.tensor_scalar(out=rows, in0=rows, scalar1=rates[0][t][:], scalar2=0.0, op0=MULT, op1=ADD)
-        unscaled10 = held([P, SLOTS, HALF], F32, "unscaled10")
-        make_post(1, 0, unscaled10)
-        wa_grouped[(0, 0)] = group_wa(0, 0, nc.scalar.copy)
+                nc.gpsimd.tensor_scalar(out=rows, in0=rows, scalar1=rates[0][t], scalar2=0.0, op0=MULT, op1=ADD)
+        post[(1, 0)] = held([P, SLOTS, HALF], F32, "post10")[:]
+        make_post(1, 0, post[(1, 0)])
+        for t in range(SLOTS):
+            rows = post[(1, 0)][:, t, :]
+            nc.gpsimd.tensor_scalar(out=rows, in0=rows, scalar1=rates[1][t], scalar2=0.0, op0=MULT, op1=ADD)
+        wa_grouped[(0, 0)] = group_wa(0, 0, [(nc.vector.tensor_copy, 0, 1), (nc.scalar.copy, 1, SLOTS)])
         unscaled = held([P, SLOTS, HALF], F32, "unscaled11", after="wa_raw00")
         make_post(1, 1, unscaled)
 
-        wa_grouped[(1, 0)] = group_wa(1, 0, nc.vector.tensor_copy)
+        wa_grouped[(1, 0)] = group_wa(1, 0, on_vector)
         wa_q[(1, 0)] = quantize(wa_grouped[(1, 0)], "wa10")
         wa_q[(0, 0)] = quantize(wa_grouped[(0, 0)], "wa00", after="wa_raw10")
-        post[(1, 0)] = held([P, SLOTS, HALF], F32, "post10", after="wa_grouped00")[:]
-        scale_post(post[(1, 0)], unscaled10, 1)
-        wa_grouped[(0, 1)] = group_wa(0, 1, nc.vector.tensor_copy)
+        wa_grouped[(0, 1)] = group_wa(0, 1, on_vector)
         post[(1, 1)] = held([P, SLOTS, HALF], F32, "post11", after="wa_raw01")[:]
         scale_post(post[(1, 1)], unscaled, 1)
         wa_q[(0, 1)] = quantize(wa_grouped[(0, 1)], "wa01")
-        wa_grouped[(1, 1)] = group_wa(1, 1, nc.vector.tensor_copy)
+        wa_grouped[(1, 1)] = group_wa(1, 1, on_vector)
         wa_q[(1, 1)] = quantize(wa_grouped[(1, 1)], "wa11")
 
         def make_pre(b, jh, after=None):
             pre = held([P, SLOTS, HALF], F32, "pre%d%d" % (b, jh), after)
             order = (1 - b, b)
-            for t in range(SLOTS):
-                acc = next_bank()
+            accs = [next_bank() for t in range(SLOTS)]
+            for u in range(WARM_UPS if (b, jh) == (0, 0) else 0):
+                nc.tensor.matmul_mx(
+                    out=accs[-1][:],
+                    lhsT=v_w[0][0][:, 0:P].bitcast(FP8X4),
+                    lhsT_scale=v_s[0][4:P, 0:P],
+                    rhs=v_w[0][0].bitcast(FP8X4),
+                    rhs_scale=v_s[0][4:P, :],
+                    start=True,
+                    stop=True,
+                )
+            for t, acc in enumerate(accs):
                 for a in order:
                     codes, scales = wa_q[(a, b)]
                     nc.tensor.matmul_mx(
@@ -257,12 +270,12 @@ def tile_list_hebbian_trace_update_kernel(
         for jh in range(2):
             h_q[(0, jh)] = quantize(h_grouped[(0, jh)], "h0%d" % jh)
         w_grouped = [group_w(0, "wa_grouped01", [nc.scalar.copy])]
-        h_grouped[(1, 0)] = make_h(make_pre(1, 0, after="w_raw0"), 1, 0, after="h_grouped00")
         w_q[0] = quantize(w_grouped[0], "w0")
+        h_grouped[(1, 0)] = make_h(make_pre(1, 0, after="w_raw0"), 1, 0, after="h_grouped00")
         w_grouped.append(group_w(1, "wa_grouped10", [nc.scalar.copy]))
         h_q[(1, 0)] = quantize(h_grouped[(1, 0)], "h10")
         w_q[1] = quantize(w_grouped[1], "w1")
-        h_grouped[(1, 1)] = make_h(make_pre(1, 1, after="pre00"), 1, 1, after="h_grouped01")
+        h_grouped[(1, 1)] = make_h(make_pre(1, 1, after="w_raw1"), 1, 1, after="h_grouped01")
 
         sums = [held([P, S], F32, "sums%d" % q) for q in range(N // P)]
 

@@ -59,8 +59,7 @@ def tile_list_hebbian_trace_update_kernel(
         wb_s_raw = held([P, H // 4], I32, "wb_s_raw")
         wb_w = held([P, H // 2], I32, "wb_w")
         wb_s = held([P, H // 4], I32, "wb_s")
-        rate_runs = held([P, 2, 16], F32, "rate_runs")
-        rates = [[rate_runs[:, b, RUN * t : RUN * t + 1] for t in range(SLOTS)] for b in range(2)]
+        rates = [[held([P, 1], F32, "rates%d%d" % (b, t)) for t in range(SLOTS)] for b in range(2)]
 
         nc.vector.memset(tab2_s[:], 0)
         nc.vector.memset(tab_s[:], 0)
@@ -79,10 +78,10 @@ def tile_list_hebbian_trace_update_kernel(
             for t in range(SLOTS):
                 nc.sync.dma_start(out=w_raw[b][:, t, :], in_=rows[t])
 
-        def load_rates():
-            groups = eta.rearrange("(b m x) -> m b x", b=2, x=16)
-            for i in range(RUN):
-                nc.sync.dma_start(out=rate_runs[i:P:RUN, :, 0:13], in_=groups[:, :, i : i + 13])
+        def load_rates(b, slots):
+            values = eta[b * PASS : (b + 1) * PASS].rearrange("(m t i) -> t m i", t=SLOTS, i=RUN)
+            for t in slots:
+                nc.sync.dma_start(out=rates[b][t][:], in_=values[t])
 
         def load_words(dst, words):
             nc.sync.dma_start(out=dst[:], in_=words.rearrange("p t i -> p (t i)").bitcast(I32))
@@ -109,13 +108,15 @@ def tile_list_hebbian_trace_update_kernel(
         nc.sync.dma_start(list1[:], offs)
         load_plane(wb_s_raw, wb_scales[0])
         load_words(tab_w[0], tab_words[0])
-        load_rates()
+        load_rates(0, range(SLOTS))
         load_tab_planes([0])
         load_words(tab_w[1], tab_words[1])
         load_tab_planes([1, 2, 3])
         load_wa(0, 0)
+        load_rates(1, [0])
         load_wa(1, 0)
         load_wa(0, 1)
+        load_rates(1, range(1, SLOTS))
         load_wa(1, 1)
         load_w(0, after="tab2_w")
         load_w(1, after="tab_w0")
@@ -164,63 +165,75 @@ def tile_list_hebbian_trace_update_kernel(
             out=wb_w[:].rearrange("p (t m e) -> p t m e", t=SLOTS, e=2),
             in_=wb_w_raw[:].rearrange("p (m t e) -> p t m e", t=SLOTS, e=2),
         )
-        v2_s = halves(gather(tab2_s[:].bitcast(U8), list2[:], U8, "v2_s"))
+        v2_s = gather(tab2_s[:].bitcast(U8), list2[:], U8, "v2_s")
         nc.vector.tensor_copy(
             out=wb_s[:].rearrange("p (t m) -> p t m", t=SLOTS),
             in_=wb_s_raw[:].rearrange("p (m t) -> p t m", t=SLOTS),
         )
-        v2_w = [
-            gather(tab2_w[:].bitcast(U32), half_of(list2, jh), U32, "v2_w%d" % jh, after)[:]
-            for jh, after in enumerate([None, "wb_s_raw"])
-        ]
+        pieces = [(0, HALF, None), (HALF, HALF, "wb_s_raw")]
+        v2_w = {}
+        for first, width, after in pieces:
+            offsets = list2[:, first // LIST_ROWS : (first + width) // LIST_ROWS]
+            v2_w[first] = gather(tab2_w[:].bitcast(U32), offsets, U32, "v2_w%d" % first, after)
         v_w = [halves(gather(tab_w[a][:].bitcast(U32), list1[:], U32, "v_w%d" % a)) for a in range(2)]
         v_s = halves(gather(tab_s[:].bitcast(U8), list1[:], U8, "v_s"))
 
-        def make_post(b, jh, dst):
-            for t in range(SLOTS):
-                acc = next_bank()
-                col = (2 * t + b) * P
+        def post_sum(b, t, some_pieces, acc, origin):
+            col = (2 * t + b) * P
+            for first, width, after in some_pieces:
                 nc.tensor.matmul_mx(
-                    out=acc[:],
+                    out=acc[:, first - origin : first - origin + width],
                     lhsT=wb_w[:].bitcast(U8)[:, 2 * col : 2 * (col + P)].bitcast(FP4X4),
                     lhsT_scale=wb_s[:].bitcast(U8)[:, col : col + P],
-                    rhs=v2_w[jh].bitcast(FP8X4),
-                    rhs_scale=v2_s[jh],
+                    rhs=v2_w[first][:].bitcast(FP8X4),
+                    rhs_scale=v2_s[:, first : first + width],
                     start=True,
                     stop=True,
                 )
-                nc.scalar.activation(out=dst[:, t, :], in_=acc[:], func=TANH)
 
-        def scale_post(dst, src, b):
-            for t in range(SLOTS):
-                nc.vector.tensor_scalar(
-                    out=dst[:, t, :], in0=src[:, t, :], scalar1=rates[b][t], scalar2=None, op0=MULT
-                )
+        def make_post(b, t, some_pieces, dst):
+            acc = next_bank()
+            origin = some_pieces[0][0]
+            width = sum(piece[1] for piece in some_pieces)
+            post_sum(b, t, some_pieces, acc, origin)
+            nc.scalar.activation(out=dst[:, origin : origin + width], in_=acc[:, 0:width], func=TANH)
+
+        def scale_on_gpsimd(rows, rate):
+            nc.gpsimd.tensor_scalar(out=rows, in0=rows, scalar1=rate[:], scalar2=0.0, op0=MULT, op1=ADD)
 
         post, wa_grouped, wa_q = {}, {}, {}
         on_vector = [(nc.vector.tensor_copy, 0, SLOTS)]
-        both = held([P, SLOTS, S], F32, "post0")
-        for jh in range(2):
-            post[(0, jh)] = both[:, :, jh * HALF : (jh + 1) * HALF]
-            make_post(0, jh, post[(0, jh)])
+        post_of_pass = [held([P, SLOTS, S], F32, "post%d" % b) for b in range(2)]
+        for b in range(2):
+            for jh in range(2):
+                post[(b, jh)] = post_of_pass[b][:, :, jh * HALF : (jh + 1) * HALF]
+        by_half = [pieces[0:1], pieces[1:2]]
+        for piece in pieces:
             for t in range(SLOTS):
-                rows = post[(0, jh)][:, t, :]
-                nc.gpsimd.tensor_scalar(out=rows, in0=rows, scalar1=rates[0][t], scalar2=0.0, op0=MULT, op1=ADD)
-        post[(1, 0)] = held([P, SLOTS, HALF], F32, "post10")[:]
-        make_post(1, 0, post[(1, 0)])
-        for t in range(SLOTS):
-            rows = post[(1, 0)][:, t, :]
-            nc.gpsimd.tensor_scalar(out=rows, in0=rows, scalar1=rates[1][t], scalar2=0.0, op0=MULT, op1=ADD)
-        wa_grouped[(0, 0)] = group_wa(0, 0, [(nc.vector.tensor_copy, 0, 1), (nc.scalar.copy, 1, SLOTS)])
-        unscaled = held([P, SLOTS, HALF], F32, "unscaled11", after="wa_raw00")
-        make_post(1, 1, unscaled)
+                make_post(0, t, [piece], post_of_pass[0][:, t, :])
+            for t in range(SLOTS):
+                scale_on_gpsimd(post[(0, piece[0] // HALF)][:, t, :], rates[0][t])
+        for jh in range(2):
+            make_post(1, 0, by_half[jh], post_of_pass[1][:, 0, :])
+            scale_on_gpsimd(post[(1, jh)][:, 0, :], rates[1][0])
+        wa_grouped[(0, 0)] = group_wa(0, 0, [(nc.scalar.copy, 0, SLOTS)])
+        unscaled = held([P, SLOTS - 1, S], F32, "unscaled", after="wa_raw00")
+        for t in range(1, SLOTS):
+            for jh in range(2):
+                make_post(1, t, by_half[jh], unscaled[:, t - 1, :])
+
+        def scale_on_vector(t):
+            nc.vector.tensor_scalar(
+                out=post_of_pass[1][:, t, :], in0=unscaled[:, t - 1, :], scalar1=rates[1][t][:], scalar2=None, op0=MULT
+            )
 
         wa_grouped[(1, 0)] = group_wa(1, 0, on_vector)
         wa_q[(1, 0)] = quantize(wa_grouped[(1, 0)], "wa10")
         wa_q[(0, 0)] = quantize(wa_grouped[(0, 0)], "wa00", after="wa_raw10")
         wa_grouped[(0, 1)] = group_wa(0, 1, on_vector)
-        post[(1, 1)] = held([P, SLOTS, HALF], F32, "post11", after="wa_raw01")[:]
-        scale_post(post[(1, 1)], unscaled, 1)
+        scale_on_vector(1)
+        scale_on_vector(2)
+        scale_on_vector(3)
         wa_q[(0, 1)] = quantize(wa_grouped[(0, 1)], "wa01")
         wa_grouped[(1, 1)] = group_wa(1, 1, on_vector)
         wa_q[(1, 1)] = quantize(wa_grouped[(1, 1)], "wa11")
@@ -231,7 +244,7 @@ def tile_list_hebbian_trace_update_kernel(
             accs = [next_bank() for t in range(SLOTS)]
             for u in range(WARM_UPS if (b, jh) == (0, 0) else 0):
                 nc.tensor.matmul_mx(
-                    out=accs[-1][:],
+                    out=accs[1][:],
                     lhsT=v_w[0][0][:, 0:P].bitcast(FP8X4),
                     lhsT_scale=v_s[0][4:P, 0:P],
                     rhs=v_w[0][0].bitcast(FP8X4),

@@ -25,7 +25,7 @@ LIST_ROWS = 16
 HALF = S // 2
 RUN = 4
 PAIR = 2
-WARM_UPS = 4
+RING = 4
 BANKS = 8
 
 
@@ -43,11 +43,8 @@ def tile_list_hebbian_trace_update_kernel(
             tags[name] = tags[after] if after else name
             return sbuf.tile(shape, dtype, name=name, tag=tags[name], align_bytes=64)
 
-        banks = []
-
-        def next_bank():
-            banks.append(psum.tile([P, HALF], F32, name="acc", tag="bank%d" % (len(banks) % BANKS)))
-            return banks[-1]
+        def bank(number):
+            return psum.tile([P, HALF], F32, name="acc", tag="bank%d" % (number % BANKS))
 
         list1 = sbuf.tile([P, S // LIST_ROWS], U16, name="list1")
         list2 = sbuf.tile([P, S // LIST_ROWS], U16, name="list2")
@@ -191,8 +188,8 @@ def tile_list_hebbian_trace_update_kernel(
                     stop=True,
                 )
 
-        def make_post(b, t, some_pieces, dst):
-            acc = next_bank()
+        def make_post(b, t, some_pieces, dst, number):
+            acc = bank(number)
             origin = some_pieces[0][0]
             width = sum(piece[1] for piece in some_pieces)
             post_sum(b, t, some_pieces, acc, origin)
@@ -210,17 +207,17 @@ def tile_list_hebbian_trace_update_kernel(
         by_half = [pieces[0:1], pieces[1:2]]
         for piece in pieces:
             for t in range(SLOTS):
-                make_post(0, t, [piece], post_of_pass[0][:, t, :])
+                make_post(0, t, [piece], post_of_pass[0][:, t, :], SLOTS * (piece[0] // HALF) + t)
             for t in range(SLOTS):
                 scale_on_gpsimd(post[(0, piece[0] // HALF)][:, t, :], rates[0][t])
         for jh in range(2):
-            make_post(1, 0, by_half[jh], post_of_pass[1][:, 0, :])
+            make_post(1, 0, by_half[jh], post_of_pass[1][:, 0, :], jh)
             scale_on_gpsimd(post[(1, jh)][:, 0, :], rates[1][0])
         wa_grouped[(0, 0)] = group_wa(0, 0, [(nc.scalar.copy, 0, SLOTS)])
         unscaled = held([P, SLOTS - 1, S], F32, "unscaled", after="wa_raw00")
         for t in range(1, SLOTS):
             for jh in range(2):
-                make_post(1, t, by_half[jh], unscaled[:, t - 1, :])
+                make_post(1, t, by_half[jh], unscaled[:, t - 1, :], 2 + (2 * (t - 1) + jh) % RING)
 
         def scale_on_vector(t):
             nc.vector.tensor_scalar(
@@ -241,18 +238,8 @@ def tile_list_hebbian_trace_update_kernel(
         def make_pre(b, jh, after=None):
             pre = held([P, SLOTS, HALF], F32, "pre%d%d" % (b, jh), after)
             order = (1 - b, b)
-            accs = [next_bank() for t in range(SLOTS)]
-            for u in range(WARM_UPS if (b, jh) == (0, 0) else 0):
-                nc.tensor.matmul_mx(
-                    out=accs[1][:],
-                    lhsT=v_w[0][0][:, 0:P].bitcast(FP8X4),
-                    lhsT_scale=v_s[0][4:P, 0:P],
-                    rhs=v_w[0][0].bitcast(FP8X4),
-                    rhs_scale=v_s[0][4:P, :],
-                    start=True,
-                    stop=True,
-                )
-            for t, acc in enumerate(accs):
+            for t in range(SLOTS):
+                acc = bank(2 + RING + SLOTS * jh + t)
                 for a in order:
                     codes, scales = wa_q[(a, b)]
                     nc.tensor.matmul_mx(
@@ -293,7 +280,7 @@ def tile_list_hebbian_trace_update_kernel(
         sums = [held([P, S], F32, "sums%d" % q) for q in range(N // P)]
 
         def third_product(q, jh):
-            acc = next_bank()
+            acc = bank(2 + RING + SLOTS * jh + q)
             for b in range(2):
                 w_codes, w_scales = w_q[b]
                 h_codes, h_scales = h_q[(b, jh)]

@@ -25,8 +25,10 @@ LIST_ROWS = 16
 HALF = S // 2
 RUN = 4
 PAIR = 2
-RING = 4
 BANKS = 8
+RING_FIRST = 2
+RING = 4
+LATER_FIRST = RING_FIRST + RING
 
 
 def tile_list_hebbian_trace_update_kernel(
@@ -83,8 +85,8 @@ def tile_list_hebbian_trace_update_kernel(
         def load_words(dst, words):
             nc.sync.dma_start(out=dst[:], in_=words.rearrange("p t i -> p (t i)").bitcast(I32))
 
-        def load_g(q, after=None):
-            g_tab[q] = held([P, T], F32, "g_tab%d" % q, after)
+        def load_g(q):
+            g_tab[q] = held([P, T], F32, "g_tab%d" % q)
             nc.sync.dma_start(out=g_tab[q][:], in_=gT[q * P : (q + 1) * P, :])
 
         def load_plane(dst, rows):
@@ -92,12 +94,14 @@ def tile_list_hebbian_trace_update_kernel(
             for r in range(4):
                 nc.sync.dma_start(out=dst[r:P:QUADRANT, :], in_=by_place[r].bitcast(I32))
 
-        def load_tab_planes(places):
-            for r in places:
-                for a in range(2):
-                    by_place = tab_scales[a].rearrange("(u r) c -> r u c", r=4)
-                    nc.sync.dma_start(out=tab_s[4 * (a + 1) + r : P : QUADRANT, :], in_=by_place[r].bitcast(I32))
+        def load_tab_planes():
+            for u in range(P // QUADRANT):
+                first = QUADRANT * u + 4
+                nc.gpsimd.dma_start(
+                    out=tab_s[first : first + 8, :], in_=tab_scales[:, 4 * u : 4 * u + 4, :].bitcast(I32)
+                )
 
+        load_tab_planes()
         nc.sync.dma_start(out=wb_w_raw[:], in_=wb_words[0].bitcast(I32))
         nc.sync.dma_start(list2[:], offs2)
         load_plane(tab2_s, tab2_scales[0])
@@ -106,9 +110,7 @@ def tile_list_hebbian_trace_update_kernel(
         load_plane(wb_s_raw, wb_scales[0])
         load_words(tab_w[0], tab_words[0])
         load_rates(0, range(SLOTS))
-        load_tab_planes([0])
         load_words(tab_w[1], tab_words[1])
-        load_tab_planes([1, 2, 3])
         load_wa(0, 0)
         load_rates(1, [0])
         load_wa(1, 0)
@@ -117,10 +119,8 @@ def tile_list_hebbian_trace_update_kernel(
         load_wa(1, 1)
         load_w(0, after="tab2_w")
         load_w(1, after="tab_w0")
-        load_g(0, after="tab_w1")
-        load_g(1)
-        load_g(2)
-        load_g(3)
+        for q in range(N // P):
+            load_g(q)
 
         half_cols = HALF // LIST_ROWS
 
@@ -136,110 +136,96 @@ def tile_list_hebbian_trace_update_kernel(
             return picked
 
         def quantize(grouped, name, after=None):
-            codes = held([P, PASS], U32, name + "_codes", after)
-            scales = held([P, PASS], U8, name + "_scales")
+            words = grouped.shape[1] // SLOTS
+            codes = held([P, words], U32, name + "_codes", after)
+            scales = held([P, words], U8, name + "_scales")
             nc.vector.quantize_mx(out=codes[:].bitcast(FP8X4), scales=scales[:], in_=grouped[:])
-            return codes, scales
+            return [(codes[:, u : u + PASS], scales[:, u : u + PASS]) for u in range(0, words, PASS)]
 
-        def group_wa(a, b, shares):
-            grouped = held([P, SLOTS * PASS], BF16, "wa_grouped%d%d" % (a, b))
-            dst = grouped[:].rearrange("p (t m i j) -> p t m j i", t=SLOTS, i=RUN, j=SLOTS)
-            src = wa_raw[(a, b)][:].rearrange("p j (m t i) -> p t m j i", t=SLOTS, i=RUN)
-            for copy, first, end in shares:
-                copy(out=dst[:, first:end], in_=src[:, first:end])
-            return grouped
+        def operand(grouped, u):
+            return grouped[:, u * SLOTS * PASS : (u + 1) * SLOTS * PASS]
 
-        def group_w(b, after, copies):
-            grouped = held([P, SLOTS * PASS], BF16, "w_grouped%d" % b, after)
-            dst = grouped[:].rearrange("p (c i t) -> p c t i", t=SLOTS, i=RUN)
-            src = w_raw[b][:].rearrange("p t (c i) -> p c t i", i=RUN)
-            share = N // RUN // len(copies)
-            for u, copy in enumerate(copies):
-                copy(out=dst[:, u * share : (u + 1) * share], in_=src[:, u * share : (u + 1) * share])
-            return grouped
+        def group_wa(a, b, dst, copy):
+            copy(
+                out=dst.rearrange("p (t m i j) -> p t m j i", t=SLOTS, i=RUN, j=SLOTS),
+                in_=wa_raw[(a, b)][:].rearrange("p j (m t i) -> p t m j i", t=SLOTS, i=RUN),
+            )
+
+        def group_w(b, dst):
+            nc.scalar.copy(
+                out=dst.rearrange("p (c i t) -> p c t i", t=SLOTS, i=RUN),
+                in_=w_raw[b][:].rearrange("p t (c i) -> p c t i", i=RUN),
+            )
 
         nc.vector.tensor_copy(
             out=wb_w[:].rearrange("p (t m e) -> p t m e", t=SLOTS, e=2),
             in_=wb_w_raw[:].rearrange("p (m t e) -> p t m e", t=SLOTS, e=2),
         )
-        v2_s = gather(tab2_s[:].bitcast(U8), list2[:], U8, "v2_s")
+        v2_s = halves(gather(tab2_s[:].bitcast(U8), list2[:], U8, "v2_s"))
         nc.vector.tensor_copy(
             out=wb_s[:].rearrange("p (t m) -> p t m", t=SLOTS),
             in_=wb_s_raw[:].rearrange("p (m t) -> p t m", t=SLOTS),
         )
-        pieces = [(0, HALF, None), (HALF, HALF, "wb_s_raw")]
-        v2_w = {}
-        for first, width, after in pieces:
-            offsets = list2[:, first // LIST_ROWS : (first + width) // LIST_ROWS]
-            v2_w[first] = gather(tab2_w[:].bitcast(U32), offsets, U32, "v2_w%d" % first, after)
+        v2_w = [
+            gather(tab2_w[:].bitcast(U32), half_of(list2, jh), U32, "v2_w%d" % jh, after)[:]
+            for jh, after in enumerate([None, "wb_s_raw"])
+        ]
         v_w = [halves(gather(tab_w[a][:].bitcast(U32), list1[:], U32, "v_w%d" % a)) for a in range(2)]
-        v_s = halves(gather(tab_s[:].bitcast(U8), list1[:], U8, "v_s"))
+        v_s = halves(gather(tab_s[:].bitcast(U8), list1[:], U8, "v_s", after="tab_w1"))
 
-        def post_sum(b, t, some_pieces, acc, origin):
-            col = (2 * t + b) * P
-            for first, width, after in some_pieces:
-                nc.tensor.matmul_mx(
-                    out=acc[:, first - origin : first - origin + width],
-                    lhsT=wb_w[:].bitcast(U8)[:, 2 * col : 2 * (col + P)].bitcast(FP4X4),
-                    lhsT_scale=wb_s[:].bitcast(U8)[:, col : col + P],
-                    rhs=v2_w[first][:].bitcast(FP8X4),
-                    rhs_scale=v2_s[:, first : first + width],
-                    start=True,
-                    stop=True,
-                )
-
-        def make_post(b, t, some_pieces, dst, number):
+        def make_post(b, t, jh, dst, number):
             acc = bank(number)
-            origin = some_pieces[0][0]
-            width = sum(piece[1] for piece in some_pieces)
-            post_sum(b, t, some_pieces, acc, origin)
-            nc.scalar.activation(out=dst[:, origin : origin + width], in_=acc[:, 0:width], func=TANH)
+            col = (2 * t + b) * P
+            nc.tensor.matmul_mx(
+                out=acc[:],
+                lhsT=wb_w[:].bitcast(U8)[:, 2 * col : 2 * (col + P)].bitcast(FP4X4),
+                lhsT_scale=wb_s[:].bitcast(U8)[:, col : col + P],
+                rhs=v2_w[jh].bitcast(FP8X4),
+                rhs_scale=v2_s[jh],
+                start=True,
+                stop=True,
+            )
+            nc.scalar.activation(out=dst, in_=acc[:], func=TANH)
 
         def scale_on_gpsimd(rows, rate):
             nc.gpsimd.tensor_scalar(out=rows, in0=rows, scalar1=rate[:], scalar2=0.0, op0=MULT, op1=ADD)
 
-        post, wa_grouped, wa_q = {}, {}, {}
-        on_vector = [(nc.vector.tensor_copy, 0, SLOTS)]
-        post_of_pass = [held([P, SLOTS, S], F32, "post%d" % b) for b in range(2)]
-        for b in range(2):
-            for jh in range(2):
-                post[(b, jh)] = post_of_pass[b][:, :, jh * HALF : (jh + 1) * HALF]
-        by_half = [pieces[0:1], pieces[1:2]]
-        for piece in pieces:
-            for t in range(SLOTS):
-                make_post(0, t, [piece], post_of_pass[0][:, t, :], SLOTS * (piece[0] // HALF) + t)
-            for t in range(SLOTS):
-                scale_on_gpsimd(post[(0, piece[0] // HALF)][:, t, :], rates[0][t])
+        wa_q = {}
+        wa0_grouped = [held([P, SLOTS * PASS], BF16, "wa_grouped%d0" % a) for a in range(2)]
+        wa1_grouped = held([P, 2 * SLOTS * PASS], BF16, "wa_grouped1")
+        post = [held([P, SLOTS, S], F32, "post%d" % b) for b in range(2)]
+
         for jh in range(2):
-            make_post(1, 0, by_half[jh], post_of_pass[1][:, 0, :], jh)
-            scale_on_gpsimd(post[(1, jh)][:, 0, :], rates[1][0])
-        wa_grouped[(0, 0)] = group_wa(0, 0, [(nc.scalar.copy, 0, SLOTS)])
+            for t in range(SLOTS):
+                make_post(0, t, jh, halves(post[0][:, t, :])[jh], SLOTS * jh + t)
+            for t in range(SLOTS):
+                scale_on_gpsimd(halves(post[0][:, t, :])[jh], rates[0][t])
+        for jh in range(2):
+            make_post(1, 0, jh, halves(post[1][:, 0, :])[jh], jh)
+        scale_on_gpsimd(post[1][:, 0, :], rates[1][0])
+
+        group_wa(0, 0, wa0_grouped[0][:], nc.scalar.copy)
         unscaled = held([P, SLOTS - 1, S], F32, "unscaled", after="wa_raw00")
         for t in range(1, SLOTS):
             for jh in range(2):
-                make_post(1, t, by_half[jh], unscaled[:, t - 1, :], 2 + (2 * (t - 1) + jh) % RING)
+                make_post(1, t, jh, halves(unscaled[:, t - 1, :])[jh], RING_FIRST + (2 * (t - 1) + jh) % RING)
 
-        def scale_on_vector(t):
+        group_wa(1, 0, wa0_grouped[1][:], nc.vector.tensor_copy)
+        wa_q[(1, 0)] = quantize(wa0_grouped[1], "wa10")[0]
+        wa_q[(0, 0)] = quantize(wa0_grouped[0], "wa00", after="wa_raw10")[0]
+        group_wa(0, 1, operand(wa1_grouped, 0), nc.vector.tensor_copy)
+        for t in range(1, SLOTS):
             nc.vector.tensor_scalar(
-                out=post_of_pass[1][:, t, :], in0=unscaled[:, t - 1, :], scalar1=rates[1][t][:], scalar2=None, op0=MULT
+                out=post[1][:, t, :], in0=unscaled[:, t - 1, :], scalar1=rates[1][t][:], scalar2=None, op0=MULT
             )
-
-        wa_grouped[(1, 0)] = group_wa(1, 0, on_vector)
-        wa_q[(1, 0)] = quantize(wa_grouped[(1, 0)], "wa10")
-        wa_q[(0, 0)] = quantize(wa_grouped[(0, 0)], "wa00", after="wa_raw10")
-        wa_grouped[(0, 1)] = group_wa(0, 1, on_vector)
-        scale_on_vector(1)
-        scale_on_vector(2)
-        scale_on_vector(3)
-        wa_q[(0, 1)] = quantize(wa_grouped[(0, 1)], "wa01")
-        wa_grouped[(1, 1)] = group_wa(1, 1, on_vector)
-        wa_q[(1, 1)] = quantize(wa_grouped[(1, 1)], "wa11")
+        group_wa(1, 1, operand(wa1_grouped, 1), nc.vector.tensor_copy)
+        wa_q[(0, 1)], wa_q[(1, 1)] = quantize(wa1_grouped, "wa1")
 
         def make_pre(b, jh, after=None):
             pre = held([P, SLOTS, HALF], F32, "pre%d%d" % (b, jh), after)
             order = (1 - b, b)
             for t in range(SLOTS):
-                acc = bank(2 + RING + SLOTS * jh + t)
+                acc = bank(LATER_FIRST + SLOTS * jh + t)
                 for a in order:
                     codes, scales = wa_q[(a, b)]
                     nc.tensor.matmul_mx(
@@ -254,33 +240,33 @@ def tile_list_hebbian_trace_update_kernel(
                 nc.scalar.activation(out=pre[:, t, :], in_=acc[:], func=TANH)
             return pre
 
-        def make_h(pre, b, jh, after):
-            grouped = held([P, SLOTS * HALF], BF16, "h_grouped%d%d" % (b, jh), after)
+        def make_h(pre, b, jh, dst):
             nc.vector.tensor_tensor(
-                out=grouped[:].rearrange("p (c i t) -> p c t i", t=SLOTS, i=PAIR),
+                out=dst.rearrange("p (c i t) -> p c t i", t=SLOTS, i=PAIR),
                 in0=pre[:].rearrange("p t (c i) -> p c t i", i=PAIR),
-                in1=post[(b, jh)].rearrange("p t (c i) -> p c t i", i=PAIR),
+                in1=post[b][:, :, jh * HALF : (jh + 1) * HALF].rearrange("p t (c i) -> p c t i", i=PAIR),
                 op=MULT,
             )
-            return grouped
 
-        h_grouped, h_q, w_q = {}, {}, {}
-        for jh, after in enumerate(["wa_raw11", "wa_grouped11"]):
-            h_grouped[(0, jh)] = make_h(make_pre(0, jh), 0, jh, after)
+        h_q, w_q = {}, {}
+        h0_grouped = held([P, 2 * SLOTS * HALF], BF16, "h0_grouped", after="wa_raw11")
         for jh in range(2):
-            h_q[(0, jh)] = quantize(h_grouped[(0, jh)], "h0%d" % jh)
-        w_grouped = [group_w(0, "wa_grouped01", [nc.scalar.copy])]
-        w_q[0] = quantize(w_grouped[0], "w0")
-        h_grouped[(1, 0)] = make_h(make_pre(1, 0, after="w_raw0"), 1, 0, after="h_grouped00")
-        w_grouped.append(group_w(1, "wa_grouped10", [nc.scalar.copy]))
-        h_q[(1, 0)] = quantize(h_grouped[(1, 0)], "h10")
-        w_q[1] = quantize(w_grouped[1], "w1")
-        h_grouped[(1, 1)] = make_h(make_pre(1, 1, after="w_raw1"), 1, 1, after="h_grouped01")
+            make_h(make_pre(0, jh), 0, jh, operand(h0_grouped, jh))
+        w0_grouped = held([P, SLOTS * N], BF16, "w0_grouped", after="wa_grouped00")
+        group_w(0, w0_grouped[:])
+        w_q[0] = quantize(w0_grouped, "w0")[0]
+        h_q[(0, 0)], h_q[(0, 1)] = quantize(h0_grouped, "h0")
+        h10_w1_grouped = held([P, 2 * SLOTS * HALF], BF16, "h10_w1_grouped", after="wa_grouped10")
+        make_h(make_pre(1, 0, after="w_raw0"), 1, 0, operand(h10_w1_grouped, 0))
+        group_w(1, operand(h10_w1_grouped, 1))
+        h_q[(1, 0)], w_q[1] = quantize(h10_w1_grouped, "h10_w1")
+        h11_grouped = held([P, SLOTS * HALF], BF16, "h11_grouped", after="h0_grouped")
+        make_h(make_pre(1, 1, after="w_raw1"), 1, 1, h11_grouped[:])
 
         sums = [held([P, S], F32, "sums%d" % q) for q in range(N // P)]
 
         def third_product(q, jh):
-            acc = bank(2 + RING + SLOTS * jh + q)
+            acc = bank(LATER_FIRST + SLOTS * jh + q)
             for b in range(2):
                 w_codes, w_scales = w_q[b]
                 h_codes, h_scales = h_q[(b, jh)]
@@ -288,8 +274,8 @@ def tile_list_hebbian_trace_update_kernel(
                     out=acc[:],
                     lhsT=w_codes[:, q * P : (q + 1) * P].bitcast(FP8X4),
                     lhsT_scale=w_scales[:, q * P : (q + 1) * P],
-                    rhs=h_codes[:].bitcast(FP8X4),
-                    rhs_scale=h_scales[:],
+                    rhs=h_codes.bitcast(FP8X4),
+                    rhs_scale=h_scales,
                     start=(b == 0),
                     stop=(b == 1),
                 )
@@ -301,13 +287,17 @@ def tile_list_hebbian_trace_update_kernel(
             nc.vector.tensor_tensor(res[:], g_tab[q][:].indirect(offsets), sums[q][:, first : first + width], ADD)
             nc.sync.dma_start(out=out[q * P : (q + 1) * P, first : first + width], in_=res[:])
 
+        last = N // P - 1
         for q in range(N // P):
             third_product(q, 0)
-            finish(q, 0, HALF)
+            if q < last:
+                finish(q, 0, HALF)
             if q == 0:
-                h_q[(1, 1)] = quantize(h_grouped[(1, 1)], "h11")
-        for q in range(N // P):
+                h_q[(1, 1)] = quantize(h11_grouped, "h11")[0]
+        third_product(last, 1)
+        finish(last, 0, S)
+        for q in range(last):
             third_product(q, 1)
-            widths = [HALF] if q < N // P - 1 else [HALF // 2, HALF // 2]
+            widths = [HALF] if q < last - 1 else [HALF // 2, HALF // 2]
             for u, width in enumerate(widths):
                 finish(q, HALF + u * width, width)

@@ -195,11 +195,17 @@ def tile_list_hebbian_trace_update_kernel(
         wa1_grouped = held([P, 2 * SLOTS * PASS], BF16, "wa_grouped1")
         post = [held([P, SLOTS, S], F32, "post%d" % b) for b in range(2)]
 
-        for jh in range(2):
-            for t in range(SLOTS):
-                make_post(0, t, jh, halves(post[0][:, t, :])[jh], SLOTS * jh + t)
-            for t in range(SLOTS):
+        def narrow(jh, first_bank):
+            for t in range(2):
+                make_post(0, t, jh, halves(post[0][:, t, :])[jh], first_bank + t)
                 scale_on_gpsimd(halves(post[0][:, t, :])[jh], rates[0][t])
+
+        narrow(0, 0)
+        for t in range(2, SLOTS):
+            for jh in range(2):
+                make_post(0, t, jh, halves(post[0][:, t, :])[jh], 2 * t - 2 + jh)
+            scale_on_gpsimd(post[0][:, t, :], rates[0][t])
+        narrow(1, 6)
         for jh in range(2):
             make_post(1, 0, jh, halves(post[1][:, 0, :])[jh], jh)
         scale_on_gpsimd(post[1][:, 0, :], rates[1][0])

from contextlib import ExitStack

import concourse.mybir as mybir

K, C, H, N, T, S = 1024, 512, 1024, 512, 2048, 1024
FLOPS = 2 * S * (K * H + C * H + H * N)

F32 = mybir.dt.float32
BF16 = mybir.dt.bfloat16
I32 = mybir.dt.int32
U32 = mybir.dt.uint32
U16 = mybir.dt.uint16
U8 = mybir.dt.uint8
FP8X4 = mybir.dt.float8_e4m3fn_x4
FP4X4 = mybir.dt.float4_e2m1fn_x4
TANH = mybir.ActivationFunctionType.Tanh
MULT = mybir.AluOpType.mult
ADD = mybir.AluOpType.add

P = 128
SLOTS = 4
PASS = P * SLOTS
QUADRANT = 32
LIST_ROWS = 16
HALF = S // 2
RUN = 4
PAIR = 2
BANKS = 8
RING_FIRST = 2
RING = 4
LATER_FIRST = RING_FIRST + RING


def tile_list_hebbian_trace_update_kernel(
    tc, tab_words, tab_scales, tab2_words, tab2_scales, offs, offs2, wa, wb_words, wb_scales, eta, w, gT, out
):
    nc = tc.nc
    with ExitStack() as ctx:
        sbuf = ctx.enter_context(tc.tile_pool(name="sbuf", bufs=1))
        psum = ctx.enter_context(tc.psum_pool(name="psum", bufs=1))

        tags = {}

        def held(shape, dtype, name, after=None):
            tags[name] = tags[after] if after else name
            return sbuf.tile(shape, dtype, name=name, tag=tags[name], align_bytes=64)

        def bank(number):
            return psum.tile([P, HALF], F32, name="acc", tag="bank%d" % (number % BANKS))

        list1 = sbuf.tile([P, S // LIST_ROWS], U16, name="list1")
        list2 = sbuf.tile([P, S // LIST_ROWS], U16, name="list2")
        tab_w = [held([P, T], I32, "tab_w%d" % a) for a in range(2)]
        tab2_w = held([P, T], I32, "tab2_w")
        tab_s = held([P, T // 4], I32, "tab_s")
        tab2_s = held([P, T // 4], I32, "tab2_s")
        wb_w_raw = held([P, H // 2], I32, "wb_w_raw")
        wb_s_raw = held([P, H // 4], I32, "wb_s_raw")
        wb_w = held([P, H // 2], I32, "wb_w")
        wb_s = held([P, H // 4], I32, "wb_s")
        rates = [[held([P, 1], F32, "rates%d%d" % (b, t)) for t in range(SLOTS)] for b in range(2)]

        nc.vector.memset(tab2_s[:], 0)
        nc.vector.memset(tab_s[:], 0)
        nc.vector.memset(wb_s_raw[:], 0)

        wa_raw, w_raw, g_tab = {}, {}, {}

        def load_wa(a, b):
            wa_raw[(a, b)] = held([P, SLOTS, PASS], F32, "wa_raw%d%d" % (a, b))
            rows = wa[a * PASS : (a + 1) * PASS, b * PASS : (b + 1) * PASS]
            nc.sync.dma_start(out=wa_raw[(a, b)][:], in_=rows.rearrange("(p j) c -> p j c", j=SLOTS))

        def load_w(b, after):
            w_raw[b] = held([P, SLOTS, N], F32, "w_raw%d" % b, after)
            rows = w[b * PASS : (b + 1) * PASS, :].rearrange("(m t i) n -> t m i n", t=SLOTS, i=RUN)
            for t in range(SLOTS):
                nc.sync.dma_start(out=w_raw[b][:, t, :], in_=rows[t])

        def load_rates(b, slots):
            values = eta[b * PASS : (b + 1) * PASS].rearrange("(m t i) -> t m i", t=SLOTS, i=RUN)
            for t in slots:
                nc.sync.dma_start(out=rates[b][t][:], in_=values[t])

        def load_words(dst, words):
            nc.sync.dma_start(out=dst[:], in_=words.rearrange("p t i -> p (t i)").bitcast(I32))

        def load_g(q):
            g_tab[q] = held([P, T], F32, "g_tab%d" % q)
            nc.sync.dma_start(out=g_tab[q][:], in_=gT[q * P : (q + 1) * P, :])

        def load_plane(dst, rows):
            by_place = rows.rearrange("(u r) c -> r u c", r=4)
            for r in range(4):
                nc.sync.dma_start(out=dst[r:P:QUADRANT, :], in_=by_place[r].bitcast(I32))

        def load_tab_planes():
            for u in range(P // QUADRANT):
                first = QUADRANT * u + 4
                nc.gpsimd.dma_start(
                    out=tab_s[first : first + 8, :], in_=tab_scales[:, 4 * u : 4 * u + 4, :].bitcast(I32)
                )

        load_tab_planes()
        nc.sync.dma_start(out=wb_w_raw[:], in_=wb_words[0].bitcast(I32))
        nc.sync.dma_start(list2[:], offs2)
        load_plane(tab2_s, tab2_scales[0])
        load_words(tab2_w, tab2_words[0])
        nc.sync.dma_start(list1[:], offs)
        load_plane(wb_s_raw, wb_scales[0])
        load_words(tab_w[0], tab_words[0])
        load_rates(0, range(SLOTS))
        load_words(tab_w[1], tab_words[1])
        load_wa(0, 0)
        load_rates(1, [0])
        load_wa(1, 0)
        load_wa(0, 1)
        load_rates(1, range(1, SLOTS))
        load_wa(1, 1)
        load_w(0, after="tab2_w")
        load_w(1, after="tab_w0")
        for q in range(N // P):
            load_g(q)

        half_cols = HALF // LIST_ROWS

        def half_of(offsets, jh):
            return offsets[:, jh * half_cols : (jh + 1) * half_cols]

        def halves(tile):
            return [tile[:, 0:HALF], tile[:, HALF:S]]

        def gather(window, offsets, dtype, name, after=None):
            picked = held([P, offsets.shape[1] * LIST_ROWS], dtype, name, after)
            nc.vector.tensor_copy(picked[:], window.indirect(offsets))
            return picked

        def quantize(grouped, name, after=None):
            words = grouped.shape[1] // SLOTS
            codes = held([P, words], U32, name + "_codes", after)
            scales = held([P, words], U8, name + "_scales")
            nc.vector.quantize_mx(out=codes[:].bitcast(FP8X4), scales=scales[:], in_=grouped[:])
            return [(codes[:, u : u + PASS], scales[:, u : u + PASS]) for u in range(0, words, PASS)]

        def operand(grouped, u):
            return grouped[:, u * SLOTS * PASS : (u + 1) * SLOTS * PASS]

        def group_wa(a, b, dst, copy):
            copy(
                out=dst.rearrange("p (t m i j) -> p t m j i", t=SLOTS, i=RUN, j=SLOTS),
                in_=wa_raw[(a, b)][:].rearrange("p j (m t i) -> p t m j i", t=SLOTS, i=RUN),
            )

        def group_w(b, dst):
            nc.scalar.copy(
                out=dst.rearrange("p (c i t) -> p c t i", t=SLOTS, i=RUN),
                in_=w_raw[b][:].rearrange("p t (c i) -> p c t i", i=RUN),
            )

        nc.vector.tensor_copy(
            out=wb_w[:].rearrange("p (t m e) -> p t m e", t=SLOTS, e=2),
            in_=wb_w_raw[:].rearrange("p (m t e) -> p t m e", t=SLOTS, e=2),
        )
        v2_s = halves(gather(tab2_s[:].bitcast(U8), list2[:], U8, "v2_s"))
        nc.vector.tensor_copy(
            out=wb_s[:].rearrange("p (t m) -> p t m", t=SLOTS),
            in_=wb_s_raw[:].rearrange("p (m t) -> p t m", t=SLOTS),
        )
        v2_w = [
            gather(tab2_w[:].bitcast(U32), half_of(list2, jh), U32, "v2_w%d" % jh, after)[:]
            for jh, after in enumerate([None, "wb_s_raw"])
        ]
        v_w = [halves(gather(tab_w[a][:].bitcast(U32), list1[:], U32, "v_w%d" % a)) for a in range(2)]
        v_s = halves(gather(tab_s[:].bitcast(U8), list1[:], U8, "v_s", after="tab_w1"))

        def make_post(b, t, jh, dst, number):
            acc = bank(number)
            col = (2 * t + b) * P
            nc.tensor.matmul_mx(
                out=acc[:],
                lhsT=wb_w[:].bitcast(U8)[:, 2 * col : 2 * (col + P)].bitcast(FP4X4),
                lhsT_scale=wb_s[:].bitcast(U8)[:, col : col + P],
                rhs=v2_w[jh].bitcast(FP8X4),
                rhs_scale=v2_s[jh],
                start=True,
                stop=True,
            )
            nc.scalar.activation(out=dst, in_=acc[:], func=TANH)

        def scale_on_gpsimd(rows, rate):
            nc.gpsimd.tensor_scalar(out=rows, in0=rows, scalar1=rate[:], scalar2=0.0, op0=MULT, op1=ADD)

        wa_q = {}
        wa0_grouped = [held([P, SLOTS * PASS], BF16, "wa_grouped%d0" % a) for a in range(2)]
        wa1_grouped = held([P, 2 * SLOTS * PASS], BF16, "wa_grouped1")
        post = [held([P, SLOTS, S], F32, "post%d" % b) for b in range(2)]

        def narrow(jh, first_bank):
            for t in range(2):
                make_post(0, t, jh, halves(post[0][:, t, :])[jh], first_bank + t)
                scale_on_gpsimd(halves(post[0][:, t, :])[jh], rates[0][t])

        narrow(0, 0)
        for t in range(2, SLOTS):
            for jh in range(2):
                make_post(0, t, jh, halves(post[0][:, t, :])[jh], 2 * t - 2 + jh)
            scale_on_gpsimd(post[0][:, t, :], rates[0][t])
        narrow(1, 6)
        for jh in range(2):
            make_post(1, 0, jh, halves(post[1][:, 0, :])[jh], jh)
        scale_on_gpsimd(post[1][:, 0, :], rates[1][0])

        group_wa(0, 0, wa0_grouped[0][:], nc.scalar.copy)
        unscaled = held([P, SLOTS - 1, S], F32, "unscaled", after="wa_raw00")
        for t in range(1, SLOTS):
            for jh in range(2):
                make_post(1, t, jh, halves(unscaled[:, t - 1, :])[jh], RING_FIRST + (2 * (t - 1) + jh) % RING)

        group_wa(1, 0, wa0_grouped[1][:], nc.vector.tensor_copy)
        wa_q[(1, 0)] = quantize(wa0_grouped[1], "wa10")[0]
        wa_q[(0, 0)] = quantize(wa0_grouped[0], "wa00", after="wa_raw10")[0]
        group_wa(0, 1, operand(wa1_grouped, 0), nc.vector.tensor_copy)
        for t in range(1, SLOTS):
            nc.vector.tensor_scalar(
                out=post[1][:, t, :], in0=unscaled[:, t - 1, :], scalar1=rates[1][t][:], scalar2=None, op0=MULT
            )
        group_wa(1, 1, operand(wa1_grouped, 1), nc.vector.tensor_copy)
        wa_q[(0, 1)], wa_q[(1, 1)] = quantize(wa1_grouped, "wa1")

        def make_pre(b, jh, after=None):
            pre = held([P, SLOTS, HALF], F32, "pre%d%d" % (b, jh), after)
            order = (1 - b, b)
            for t in range(SLOTS):
                acc = bank(LATER_FIRST + SLOTS * jh + t)
                for a in order:
                    codes, scales = wa_q[(a, b)]
                    nc.tensor.matmul_mx(
                        out=acc[:],
                        lhsT=codes[:, t * P : (t + 1) * P].bitcast(FP8X4),
                        lhsT_scale=scales[:, t * P : (t + 1) * P],
                        rhs=v_w[a][jh].bitcast(FP8X4),
                        rhs_scale=v_s[jh][4 * (a + 1) : P, :],
                        start=(a == order[0]),
                        stop=(a == order[1]),
                    )
                nc.scalar.activation(out=pre[:, t, :], in_=acc[:], func=TANH)
            return pre

        def make_h(pre, b, jh, dst):
            nc.vector.tensor_tensor(
                out=dst.rearrange("p (c i t) -> p c t i", t=SLOTS, i=PAIR),
                in0=pre[:].rearrange("p t (c i) -> p c t i", i=PAIR),
                in1=post[b][:, :, jh * HALF : (jh + 1) * HALF].rearrange("p t (c i) -> p c t i", i=PAIR),
                op=MULT,
            )

        h_q, w_q = {}, {}
        h0_grouped = held([P, 2 * SLOTS * HALF], BF16, "h0_grouped", after="wa_raw11")
        for jh in range(2):
            make_h(make_pre(0, jh), 0, jh, operand(h0_grouped, jh))
        w0_grouped = held([P, SLOTS * N], BF16, "w0_grouped", after="wa_grouped00")
        group_w(0, w0_grouped[:])
        w_q[0] = quantize(w0_grouped, "w0")[0]
        h_q[(0, 0)], h_q[(0, 1)] = quantize(h0_grouped, "h0")
        h10_w1_grouped = held([P, 2 * SLOTS * HALF], BF16, "h10_w1_grouped", after="wa_grouped10")
        make_h(make_pre(1, 0, after="w_raw0"), 1, 0, operand(h10_w1_grouped, 0))
        group_w(1, operand(h10_w1_grouped, 1))
        h_q[(1, 0)], w_q[1] = quantize(h10_w1_grouped, "h10_w1")
        h11_grouped = held([P, SLOTS * HALF], BF16, "h11_grouped", after="h0_grouped")
        make_h(make_pre(1, 1, after="w_raw1"), 1, 1, h11_grouped[:])

        sums = [held([P, S], F32, "sums%d" % q) for q in range(N // P)]

        def third_product(q, jh):
            acc = bank(LATER_FIRST + SLOTS * jh + q)
            for b in range(2):
                w_codes, w_scales = w_q[b]
                h_codes, h_scales = h_q[(b, jh)]
                nc.tensor.matmul_mx(
                    out=acc[:],
                    lhsT=w_codes[:, q * P : (q + 1) * P].bitcast(FP8X4),
                    lhsT_scale=w_scales[:, q * P : (q + 1) * P],
                    rhs=h_codes.bitcast(FP8X4),
                    rhs_scale=h_scales,
                    start=(b == 0),
                    stop=(b == 1),
                )
            nc.scalar.copy(out=halves(sums[q])[jh], in_=acc[:])

        def finish(q, first, width):
            res = held([P, width], F32, "res%d_%d" % (q, first))
            offsets = list1[:, first // LIST_ROWS : (first + width) // LIST_ROWS]
            nc.vector.tensor_tensor(res[:], g_tab[q][:].indirect(offsets), sums[q][:, first : first + width], ADD)
            nc.sync.dma_start(out=out[q * P : (q + 1) * P, first : first + width], in_=res[:])

        last = N // P - 1
        for q in range(N // P):
            third_product(q, 0)
            if q < last:
                finish(q, 0, HALF)
            if q == 0:
                h_q[(1, 1)] = quantize(h11_grouped, "h11")[0]
        third_product(last, 1)
        finish(last, 0, S)
        for q in range(last):
            third_product(q, 1)
            widths = [HALF] if q < last - 1 else [HALF // 2, HALF // 2]
            for u, width in enumerate(widths):
                finish(q, HALF + u * width, width)
